import numpy as np
import ml_dtypes


def mxq(x, axis, fmt="e4m3"):
    dtype, down = {"e4m3": (ml_dtypes.float8_e4m3fn, 7), "e5m2": (ml_dtypes.float8_e5m2, 14)}[fmt]
    v = np.moveaxis(np.asarray(x, np.float32).astype(ml_dtypes.bfloat16).astype(np.float64), axis, -1)
    blocks = v.reshape(v.shape[:-1] + (-1, 32))
    amax = np.abs(blocks).max(-1, keepdims=True)
    byte = np.maximum(np.where(amax > 0, np.frexp(amax)[1] - 1 + 127, 0) - down, 1)
    scale = np.exp2(byte - 127.0)
    codes = (blocks / scale).astype(np.float32).astype(dtype).astype(np.float64)
    return np.moveaxis((codes * scale).reshape(v.shape), -1, axis)


WIDE = False


def mx_kscale(k):
    if not WIDE:
        return np.ones(k)
    levels = np.array([10, -10, 5, -5, 0])
    if k % 512:
        return np.exp2(np.random.permutation(np.resize(levels, k // 32))).repeat(32)
    a = np.empty((k // 512, 16))
    for p in range(k // 512):
        a[p, :8] = np.random.permutation(np.resize(levels, 8))
        for g in range(8):
            far = levels[np.abs(levels - a[p, g]) >= 10]
            a[p, g + 8] = far[np.random.randint(len(far))]
    return np.exp2(a.ravel()).repeat(32)


def f64(x):
    return np.asarray(x).astype(np.float64)


def striped(idx):
    return np.tile(idx.reshape(-1, 16).T, (8, 1)).astype(np.uint16)


def unstriped(offs):
    return offs[:16].T.reshape(-1).astype(np.int64)


E2M1 = np.array([0.0, 0.5, 1.0, 1.5, 2.0, 3.0, 4.0, 6.0, -0.0, -0.5, -1.0, -1.5, -2.0, -3.0, -4.0, -6.0])


def pack_weight(w, fmt):
    k, n = w.shape
    w = f64(np.asarray(w, np.float32).astype(ml_dtypes.bfloat16)).reshape(k // 32, 32, n)
    amax = np.abs(w).max(1)
    if fmt == "e4m3":
        byte = np.frexp(amax)[1] - 1 + 127 - 7
    else:
        mant, ex = np.frexp(amax / 6.0)
        byte = np.where(mant > 0.5, ex, ex - 1) + 127
    byte = np.clip(np.where(amax > 0, byte, 1), 1, 254)
    scaled = (w * np.exp2(127.0 - byte)[:, None, :]).reshape(k, n).astype(np.float32)
    by_word = np.ascontiguousarray(scaled.reshape(k // 512, 128, 4, n).transpose(0, 1, 3, 2))
    if fmt == "e4m3":
        words = by_word.astype(ml_dtypes.float8_e4m3fn).view(np.uint8)
    else:
        c = by_word.astype(ml_dtypes.float4_e2m1fn).view(np.uint8) & 0xF
        words = (c[..., 0::2] | (c[..., 1::2] << 4)).reshape(k // 512, 128, 2 * n)
    return np.ascontiguousarray(words), np.ascontiguousarray(byte.astype(np.uint8).reshape(k // 512, 16, n))


def unpack_weight(words, scales, fmt):
    g, _, n = scales.shape
    words = np.ascontiguousarray(words).reshape(g, 128, n, -1)
    if fmt == "e4m3":
        vals = words.view(ml_dtypes.float8_e4m3fn).astype(np.float64)
    else:
        nib = np.empty((g, 128, n, 4), np.uint8)
        nib[..., 0::2] = words & 0xF
        nib[..., 1::2] = words >> 4
        vals = E2M1[nib]
    vals = vals * np.repeat(np.exp2(scales.astype(np.float64) - 127.0), 8, axis=1)[..., None]
    return vals.transpose(0, 1, 3, 2).reshape(g * 512, n)


def relu2(v):
    return np.maximum(v, 0.0) ** 2


K, T, E, N = 512, 4096, 8, 128
COUNTS = (128, 128, 512, 640, 896, 896, 384, 512)
STARTS = np.cumsum((0,) + COUNTS)


def by_expert(wq, xq):
    return np.concatenate([wq[e].T @ xq[:, STARTS[e]:STARTS[e + 1]] for e in range(E)], axis=1)


def setup_inputs():
    n = np.random.standard_normal
    s = mx_kscale(K)[:, None]
    expert = np.random.permutation(np.repeat(np.arange(E), COUNTS))
    slot_token = np.argsort(expert, kind="stable")
    w = [pack_weight(m, "e2m1") for m in n((E, K, N)) / np.sqrt(K) / s[None]]
    return {
        "xT": (n((K, T)) * s).astype(np.float32),
        "w_words": np.stack([m[0] for m in w]),
        "w_scales": np.stack([m[1] for m in w]),
        "b": (0.3 * n((N, E))).astype(np.float32),
        "gate": np.tile(np.random.uniform(0.2, 1.0, T), (N, 1)).astype(np.float32),
        "offs": striped(slot_token),
    }


def reference(xT, w_words, w_scales, b, gate, offs):
    idx = unstriped(offs)
    w = np.stack([unpack_weight(w_words[e], w_scales[e], "e2m1") for e in range(E)])
    xq = mxq(f64(xT)[:, idx], 0, "e4m3")
    y = by_expert(w, xq)
    y = relu2(y + np.repeat(f64(b), COUNTS, axis=1))
    out = np.zeros((N, T))
    out[:, idx] = f64(gate) * y
    return out

@@ -1,0 +1,184 @@
+import concourse.mybir as mybir
+
+F32 = mybir.dt.float32
+BF16 = mybir.dt.bfloat16
+U32 = mybir.dt.uint32
+I32 = mybir.dt.int32
+U16 = mybir.dt.uint16
+U8 = mybir.dt.uint8
+FP8X4 = mybir.dt.float8_e4m3fn_x4
+FP4X4 = mybir.dt.float4_e2m1fn_x4
+RELU = mybir.ActivationFunctionType.Relu
+SQUARE = mybir.ActivationFunctionType.Square
+MULT = mybir.AluOpType.mult
+ADD = mybir.AluOpType.add
+
+P, T, E, N, K = 128, 4096, 8, 128, 512
+COUNTS = (128, 128, 512, 640, 896, 896, 384, 512)
+FLOPS = 2 * K * N * T
+CH = 512
+NCH = T // CH
+V_LACE = (0,)
+
+
+def pieces_of(c):
+    found = []
+    start = 0
+    for e in range(E):
+        lo, hi = max(start, c * CH), min(start + COUNTS[e], (c + 1) * CH)
+        start += COUNTS[e]
+        while lo < hi:
+            width = max(n for n in (128, 256, 512) if n <= hi - lo)
+            found.append((lo - c * CH, width, e))
+            lo += width
+    return found
+
+
+def spans_of(c):
+    found = []
+    start = 0
+    for e in range(E):
+        lo, hi = max(start, c * CH), min(start + COUNTS[e], (c + 1) * CH)
+        start += COUNTS[e]
+        if lo < hi:
+            found.append((lo - c * CH, hi - c * CH, e))
+    return found
+
+
+def tile_moe_rag_lin_relu2_kernel(tc, xT, w_words, w_scales, b, gate, offs, out):
+    nc = tc.nc
+    with (
+        tc.tile_pool(name="held", bufs=1) as held,
+        tc.tile_pool(name="ring", bufs=3) as ring,
+        tc.psum_pool(name="psum", bufs=4) as psum,
+    ):
+        offsets = held.tile([P, T // 16], U16, name="offsets")
+        nc.sync.dma_start(offsets[:], offs)
+
+        w_sb = held.tile([P, E, 2 * N], U8, name="w_sb", align_bytes=64)
+        ws_sb = held.tile([P, E, N], U8, name="ws_sb", align_bytes=64)
+        b_sb = held.tile([P, E], F32, name="b_sb")
+        nc.vector.memset(ws_sb[:].rearrange("p e n -> p (e n)").bitcast(I32), 0)
+
+        rows = xT.rearrange("(p j) n -> p j n", j=4)
+        loads = []
+        for h, cuts in ((0, (0, 2048, 3072, 3584, 4096)), (1, (0, 1024, 2048, 3072, 3584, 4096))):
+            for lo, hi in zip(cuts[:-1], cuts[1:]):
+                raw = held.tile([P, 2, hi - lo], F32, name="raw" + str(h) + "_" + str(lo))
+                nc.sync.dma_start(out=raw[:], in_=rows[:, 2 * h : 2 * h + 2, lo:hi])
+                loads.append((h, lo, hi, raw))
+            if h == 0:
+                for q in range(4):
+                    nc.sync.dma_start(
+                        out=ws_sb[32 * q : 32 * q + 4].bitcast(I32),
+                        in_=w_scales[:, 0, 4 * q : 4 * q + 4, :].rearrange("e q n -> q e n").bitcast(I32),
+                    )
+                nc.sync.dma_start(out=b_sb[:], in_=b)
+        nc.sync.dma_start(
+            out=w_sb[:].bitcast(I32), in_=w_words[:, 0].rearrange("e p n -> p e n").bitcast(I32)
+        )
+        gate_sb = held.tile([P, T], F32, name="gate_sb")
+        for lo in range(0, T, 1024):
+            nc.sync.dma_start(out=gate_sb[:, lo : lo + 1024], in_=gate[:, lo : lo + 1024])
+
+        pairs = [held.tile([P, T, 2], BF16, name="pairs" + str(h), align_bytes=64) for h in (0, 1)]
+        window = [t[:].rearrange("p n e -> p (n e)").bitcast(U32) for t in pairs]
+        mates = [held.tile([P, 2, 4 * CH, 2], BF16, name="mates" + str(i), align_bytes=64) for i in range(NCH // 4)]
+        result = held.tile([P, T], F32, name="result")
+
+        def cast(load, cuts):
+            h, lo, hi, raw = load
+            bounds = (0,) + cuts + (hi - lo,)
+            for i in range(3):
+                a, z = bounds[i], bounds[i + 1]
+                if a < z:
+                    dst = pairs[h][:, lo + a : lo + z, :]
+                    src = raw[:, :, a:z].rearrange("p e n -> p n e")
+                    if i == 0:
+                        nc.vector.tensor_copy(out=dst, in_=src)
+                    elif i == 1:
+                        nc.scalar.copy(out=dst, in_=src)
+                    else:
+                        nc.gpsimd.tensor_scalar(dst, src, 1.0, 0.0, MULT, ADD)
+
+        def gather(h, lo, hi):
+            i, at = lo // (4 * CH), lo % (4 * CH)
+            nc.vector.tensor_copy(
+                out=mates[i][:, h, at : at + hi - lo, :].rearrange("p n e -> p (n e)").bitcast(U32),
+                in_=window[h].indirect(offsets[:, lo // 16 : hi // 16]),
+            )
+
+        laced = {}
+        codes = {}
+        squares = {}
+
+        def lace(c):
+            i, at = c // 4, (c % 4) * CH
+            x4 = ring.tile([P, CH, 2, 2], BF16, name="x4", align_bytes=64)
+            src = mates[i][:, :, at : at + CH, :].rearrange("p h n e -> p n h e")
+            if c in V_LACE:
+                nc.vector.tensor_copy(out=x4[:], in_=src)
+            else:
+                nc.scalar.copy(out=x4[:], in_=src)
+            laced[c] = x4
+
+        def quantise(c):
+            cw = ring.tile([P, CH], U32, name="cw", align_bytes=64)
+            cs = ring.tile([P, CH], U8, name="cs", align_bytes=64)
+            nc.vector.quantize_mx(
+                out=cw[:].bitcast(FP8X4), scales=cs[:], in_=laced[c][:].rearrange("p n h e -> p (n h e)")
+            )
+            codes[c] = (cw, cs)
+
+        def multiply(c):
+            cw, cs = codes[c]
+            bank = psum.tile([N, CH], F32, name="bank")
+            for at, width, e in pieces_of(c):
+                nc.tensor.matmul_mx(
+                    out=bank[:, at : at + width],
+                    lhsT=w_sb[:, e, :].bitcast(FP4X4),
+                    lhsT_scale=ws_sb[:, e, :],
+                    rhs=cw[:, at : at + width].bitcast(FP8X4),
+                    rhs_scale=cs[:, at : at + width],
+                    start=True,
+                    stop=True,
+                )
+            relu = ring.tile([N, CH], F32, name="relu")
+            for lo, hi, e in spans_of(c):
+                nc.scalar.activation(relu[:, lo:hi], bank[:, lo:hi], RELU, bias=b_sb[:, e : e + 1])
+            square = ring.tile([N, CH], F32, name="square")
+            nc.scalar.activation(square[:], relu[:], SQUARE)
+            squares[c] = square
+
+        def scatter(c):
+            cols = slice(c * CH, (c + 1) * CH)
+            nc.vector.tensor_tensor(
+                result[:].indirect(offsets[:, c * CH // 16 : (c + 1) * CH // 16]), squares[c][:], gate_sb[:, cols], MULT
+            )
+
+        cast(loads[0], (1280, 2048))
+        cast(loads[1], (704, 1024))
+        for load in loads[2:4]:
+            cast(load, (320, 512))
+        for load in loads[4:6]:
+            cast(load, (0, 768))
+        cast(loads[6], (0, 640))
+        cast(loads[7], (0, 288))
+        gather(0, 0, 2048)
+        gather(0, 2048, 4096)
+        cast(loads[8], (160, 384))
+
+        for step in range(NCH + 4):
+            if step in (0, 1):
+                gather(1, step * CH, (step + 1) * CH)
+            if step in (2, 4, 6):
+                gather(1, step * CH, (step + 2) * CH)
+            if 0 <= step - 1 < NCH:
+                lace(step - 1)
+            if 0 <= step - 2 < NCH:
+                quantise(step - 2)
+                multiply(step - 2)
+            if 0 <= step - 4 < NCH:
+                scatter(step - 4)
+        for queue, lo in ((nc.sync, 0), (nc.scalar, 2048)):
+            queue.dma_start(out=out[:, lo : lo + 2048], in_=result[:, lo : lo + 2048])

@@ -9,16 +9,15 @@ U8 = mybir.dt.uint8
 FP8X4 = mybir.dt.float8_e4m3fn_x4
 FP4X4 = mybir.dt.float4_e2m1fn_x4
 RELU = mybir.ActivationFunctionType.Relu
+COPY = mybir.ActivationFunctionType.Copy
 SQUARE = mybir.ActivationFunctionType.Square
 MULT = mybir.AluOpType.mult
-ADD = mybir.AluOpType.add
 
 P, T, E, N, K = 128, 4096, 8, 128, 512
 COUNTS = (128, 128, 512, 640, 896, 896, 384, 512)
 FLOPS = 2 * K * N * T
 CH = 512
 NCH = T // CH
-V_LACE = (0,)
 
 
 def pieces_of(c):
@@ -45,6 +44,11 @@ def spans_of(c):
     return found
 
 
+V_LACE = (0,)
+EARLY = 6
+V_PLANE = (6, 7)
+
+
 def tile_moe_rag_lin_relu2_kernel(tc, xT, w_words, w_scales, b, gate, offs, out):
     nc = tc.nc
     with (
@@ -53,27 +57,35 @@ def tile_moe_rag_lin_relu2_kernel(tc, xT, w_words, w_scales, b, gate, offs, out)
         tc.psum_pool(name="psum", bufs=4) as psum,
     ):
         offsets = held.tile([P, T // 16], U16, name="offsets")
-        nc.sync.dma_start(offsets[:], offs)
-
         w_sb = held.tile([P, E, 2 * N], U8, name="w_sb", align_bytes=64)
         ws_sb = held.tile([P, E, N], U8, name="ws_sb", align_bytes=64)
         b_sb = held.tile([P, E], F32, name="b_sb")
         nc.vector.memset(ws_sb[:].rearrange("p e n -> p (e n)").bitcast(I32), 0)
 
         rows = xT.rearrange("(p j) n -> p j n", j=4)
-        loads = []
-        for h, cuts in ((0, (0, 2048, 3072, 3584, 4096)), (1, (0, 1024, 2048, 3072, 3584, 4096))):
+
+        def load(first, count, cuts):
+            found = []
             for lo, hi in zip(cuts[:-1], cuts[1:]):
-                raw = held.tile([P, 2, hi - lo], F32, name="raw" + str(h) + "_" + str(lo))
-                nc.sync.dma_start(out=raw[:], in_=rows[:, 2 * h : 2 * h + 2, lo:hi])
-                loads.append((h, lo, hi, raw))
-            if h == 0:
-                for q in range(4):
-                    nc.sync.dma_start(
-                        out=ws_sb[32 * q : 32 * q + 4].bitcast(I32),
-                        in_=w_scales[:, 0, 4 * q : 4 * q + 4, :].rearrange("e q n -> q e n").bitcast(I32),
-                    )
-                nc.sync.dma_start(out=b_sb[:], in_=b)
+                raw = held.tile([P, count, hi - lo], F32, name="raw" + str(first) + "_" + str(lo))
+                nc.sync.dma_start(out=raw[:], in_=rows[:, first : first + count, lo:hi])
+                found.append((lo, hi, raw))
+            return found
+
+        raw2 = held.tile([P, T], F32, name="raw2")
+        cuts2 = (0, 2048, 3840, 4096)
+        for lo, hi in zip(cuts2[:-1], cuts2[1:]):
+            nc.sync.dma_start(out=raw2[:, lo:hi], in_=rows[:, 2, lo:hi])
+            if lo == 0:
+                nc.sync.dma_start(offsets[:], offs)
+        raw01 = load(0, 2, (0, 1024, 2048, 3072, 3840, 4096))
+        for q in range(4):
+            nc.sync.dma_start(
+                out=ws_sb[32 * q : 32 * q + 4].bitcast(I32),
+                in_=w_scales[:, 0, 4 * q : 4 * q + 4, :].rearrange("e q n -> q e n").bitcast(I32),
+            )
+        nc.sync.dma_start(out=b_sb[:], in_=b)
+        raw3 = load(3, 1, (0, 1024, 2048, 3072, 3840, 4096))
         nc.sync.dma_start(
             out=w_sb[:].bitcast(I32), in_=w_words[:, 0].rearrange("e p n -> p e n").bitcast(I32)
         )
@@ -81,52 +93,45 @@ def tile_moe_rag_lin_relu2_kernel(tc, xT, w_words, w_scales, b, gate, offs, out)
         for lo in range(0, T, 1024):
             nc.sync.dma_start(out=gate_sb[:, lo : lo + 1024], in_=gate[:, lo : lo + 1024])
 
-        pairs = [held.tile([P, T, 2], BF16, name="pairs" + str(h), align_bytes=64) for h in (0, 1)]
-        window = [t[:].rearrange("p n e -> p (n e)").bitcast(U32) for t in pairs]
-        mates = [held.tile([P, 2, 4 * CH, 2], BF16, name="mates" + str(i), align_bytes=64) for i in range(NCH // 4)]
+        pairs = held.tile([P, T, 2], BF16, name="pairs", align_bytes=64)
+        words = pairs[:].rearrange("p n e -> p (n e)").bitcast(U32)
+        plane2 = held.tile([P, T], BF16, name="plane2", align_bytes=64)
+        plane3 = held.tile([P, T], BF16, name="plane3", align_bytes=64)
+        mates = [
+            held.tile([P, 3 if c + EARLY < NCH else 2, CH, 2], BF16, name="mates" + str(c), align_bytes=64)
+            for c in range(EARLY)
+        ]
         result = held.tile([P, T], F32, name="result")
 
-        def cast(load, cuts):
-            h, lo, hi, raw = load
-            bounds = (0,) + cuts + (hi - lo,)
-            for i in range(3):
-                a, z = bounds[i], bounds[i + 1]
-                if a < z:
-                    dst = pairs[h][:, lo + a : lo + z, :]
-                    src = raw[:, :, a:z].rearrange("p e n -> p n e")
-                    if i == 0:
-                        nc.vector.tensor_copy(out=dst, in_=src)
-                    elif i == 1:
-                        nc.scalar.copy(out=dst, in_=src)
-                    else:
-                        nc.gpsimd.tensor_scalar(dst, src, 1.0, 0.0, MULT, ADD)
+        def slots(c):
+            return offsets[:, c * CH // 16 : (c + 1) * CH // 16]
 
-        def gather(h, lo, hi):
-            i, at = lo // (4 * CH), lo % (4 * CH)
+        def gather_words(c):
             nc.vector.tensor_copy(
-                out=mates[i][:, h, at : at + hi - lo, :].rearrange("p n e -> p (n e)").bitcast(U32),
-                in_=window[h].indirect(offsets[:, lo // 16 : hi // 16]),
+                out=mates[c % EARLY][:, 0].rearrange("p n e -> p (n e)").bitcast(U32), in_=words.indirect(slots(c))
             )
+
+        def gather_plane(plane, e, c):
+            nc.scalar.activation(mates[c % EARLY][:, 1 + c // EARLY, :, e], plane[:].indirect(slots(c)), COPY)
 
         laced = {}
         codes = {}
         squares = {}
 
         def lace(c):
-            i, at = c // 4, (c % 4) * CH
-            x4 = ring.tile([P, CH, 2, 2], BF16, name="x4", align_bytes=64)
-            src = mates[i][:, :, at : at + CH, :].rearrange("p h n e -> p n h e")
-            if c in V_LACE:
-                nc.vector.tensor_copy(out=x4[:], in_=src)
-            else:
-                nc.scalar.copy(out=x4[:], in_=src)
+            x4 = ring.tile([P, CH, 4], BF16, name="x4", align_bytes=64)
+            engine, word = (nc.vector.tensor_copy, I32) if c in V_LACE else (nc.scalar.copy, U32)
+            both = mates[c % EARLY][:].rearrange("p h n e -> p h (n e)").bitcast(word)
+            src = both[:, 0 : 2 + c // EARLY : 1 + c // EARLY, :].rearrange("p h n -> p n h")
+            dst = x4[:].rearrange("p n t -> p (n t)").bitcast(word).rearrange("p (n h) -> p n h", h=2)
+            engine(out=dst, in_=src)
             laced[c] = x4
 
         def quantise(c):
             cw = ring.tile([P, CH], U32, name="cw", align_bytes=64)
             cs = ring.tile([P, CH], U8, name="cs", align_bytes=64)
             nc.vector.quantize_mx(
-                out=cw[:].bitcast(FP8X4), scales=cs[:], in_=laced[c][:].rearrange("p n h e -> p (n h e)")
+                out=cw[:].bitcast(FP8X4), scales=cs[:], in_=laced[c][:].rearrange("p n t -> p (n t)")
             )
             codes[c] = (cw, cs)
 
@@ -151,34 +156,34 @@ def tile_moe_rag_lin_relu2_kernel(tc, xT, w_words, w_scales, b, gate, offs, out)
             squares[c] = square
 
         def scatter(c):
-            cols = slice(c * CH, (c + 1) * CH)
             nc.vector.tensor_tensor(
-                result[:].indirect(offsets[:, c * CH // 16 : (c + 1) * CH // 16]), squares[c][:], gate_sb[:, cols], MULT
+                result[:].indirect(slots(c)), squares[c][:], gate_sb[:, c * CH : (c + 1) * CH], MULT
             )
 
-        cast(loads[0], (1280, 2048))
-        cast(loads[1], (704, 1024))
-        for load in loads[2:4]:
-            cast(load, (320, 512))
-        for load in loads[4:6]:
-            cast(load, (0, 768))
-        cast(loads[6], (0, 640))
-        cast(loads[7], (0, 288))
-        gather(0, 0, 2048)
-        gather(0, 2048, 4096)
-        cast(loads[8], (160, 384))
+        for lo, hi in zip(cuts2[:-1], cuts2[1:]):
+            nc.vector.tensor_copy(out=plane2[:, lo:hi], in_=raw2[:, lo:hi])
+        for c in range(NCH):
+            if c in V_PLANE:
+                nc.vector.tensor_copy(out=mates[c % EARLY][:, 1 + c // EARLY, :, 0], in_=raw2[:].indirect(slots(c)))
+            else:
+                gather_plane(plane2, 0, c)
+        for lo, hi, raw in raw01:
+            nc.vector.tensor_copy(out=pairs[:, lo:hi, :], in_=raw[:].rearrange("p e n -> p n e"))
+        for lo, hi, raw in raw3:
+            nc.scalar.copy(out=plane3[:, lo:hi], in_=raw[:, 0])
+        for c in range(EARLY):
+            gather_words(c)
 
-        for step in range(NCH + 4):
-            if step in (0, 1):
-                gather(1, step * CH, (step + 1) * CH)
-            if step in (2, 4, 6):
-                gather(1, step * CH, (step + 2) * CH)
+        for step in range(NCH + 3):
+            if step < NCH:
+                gather_plane(plane3, 1, step)
+                lace(step)
             if 0 <= step - 1 < NCH:
-                lace(step - 1)
-            if 0 <= step - 2 < NCH:
-                quantise(step - 2)
-                multiply(step - 2)
-            if 0 <= step - 4 < NCH:
-                scatter(step - 4)
+                quantise(step - 1)
+                multiply(step - 1)
+            if EARLY <= step - 1 + EARLY < NCH:
+                gather_words(step - 1 + EARLY)
+            if 0 <= step - 3 < NCH:
+                scatter(step - 3)
         for queue, lo in ((nc.sync, 0), (nc.scalar, 2048)):
             queue.dma_start(out=out[:, lo : lo + 2048], in_=result[:, lo : lo + 2048])

@@ -12,6 +12,7 @@ RELU = mybir.ActivationFunctionType.Relu
 COPY = mybir.ActivationFunctionType.Copy
 SQUARE = mybir.ActivationFunctionType.Square
 MULT = mybir.AluOpType.mult
+ADD = mybir.AluOpType.add
 
 P, T, E, N, K = 128, 4096, 8, 128, 512
 COUNTS = (128, 128, 512, 640, 896, 896, 384, 512)
@@ -39,14 +40,23 @@ def spans_of(c):
     for e in range(E):
         lo, hi = max(start, c * CH), min(start + COUNTS[e], (c + 1) * CH)
         start += COUNTS[e]
-        if lo < hi:
+        if hi - lo == CH:
+            found.extend([(0, CH // 2, e), (CH // 2, CH, e)])
+        elif lo < hi:
             found.append((lo - c * CH, hi - c * CH, e))
     return found
 
 
-V_LACE = (0,)
-EARLY = 6
-V_PLANE = (6, 7)
+V_FROM = (3, 3, 4)
+V_LACE = 4
+V_LAST = 1
+CUTS = (
+    (0, 2048, 3840, 4096),
+    (0, 1024, 2048, 3072, 4096),
+    (0, 1024, 2048, 3072, 4096),
+    (0, 1024, 2048, 3072, 3840, 4096),
+)
+POOL_SHARE = {1024: 1024, 2048: 1024, 3072: 640, 3840: 384}
 
 
 def tile_moe_rag_lin_relu2_kernel(tc, xT, w_words, w_scales, b, gate, offs, out):
@@ -64,67 +74,64 @@ def tile_moe_rag_lin_relu2_kernel(tc, xT, w_words, w_scales, b, gate, offs, out)
 
         rows = xT.rearrange("(p j) n -> p j n", j=4)
 
-        def load(first, count, cuts):
+        raws = []
+        for j in range(4):
             found = []
-            for lo, hi in zip(cuts[:-1], cuts[1:]):
-                raw = held.tile([P, count, hi - lo], F32, name="raw" + str(first) + "_" + str(lo))
-                nc.sync.dma_start(out=raw[:], in_=rows[:, first : first + count, lo:hi])
+            for lo, hi in zip(CUTS[j][:-1], CUTS[j][1:]):
+                raw = held.tile([P, hi - lo], F32, name="raw" + str(j) + "_" + str(lo))
+                nc.sync.dma_start(out=raw[:], in_=rows[:, j, lo:hi])
                 found.append((lo, hi, raw))
-            return found
-
-        raw2 = held.tile([P, T], F32, name="raw2")
-        cuts2 = (0, 2048, 3840, 4096)
-        for lo, hi in zip(cuts2[:-1], cuts2[1:]):
-            nc.sync.dma_start(out=raw2[:, lo:hi], in_=rows[:, 2, lo:hi])
-            if lo == 0:
-                nc.sync.dma_start(offsets[:], offs)
-        raw01 = load(0, 2, (0, 1024, 2048, 3072, 3840, 4096))
+                if j == 0 and lo == 0:
+                    nc.sync.dma_start(offsets[:], offs)
+            raws.append(found)
+        nc.sync.dma_start(
+            out=w_sb[:].bitcast(I32), in_=w_words[:, 0].rearrange("e p n -> p e n").bitcast(I32)
+        )
         for q in range(4):
             nc.sync.dma_start(
                 out=ws_sb[32 * q : 32 * q + 4].bitcast(I32),
                 in_=w_scales[:, 0, 4 * q : 4 * q + 4, :].rearrange("e q n -> q e n").bitcast(I32),
             )
         nc.sync.dma_start(out=b_sb[:], in_=b)
-        raw3 = load(3, 1, (0, 1024, 2048, 3072, 3840, 4096))
-        nc.sync.dma_start(
-            out=w_sb[:].bitcast(I32), in_=w_words[:, 0].rearrange("e p n -> p e n").bitcast(I32)
-        )
         gate_sb = held.tile([P, T], F32, name="gate_sb")
         for lo in range(0, T, 1024):
             nc.sync.dma_start(out=gate_sb[:, lo : lo + 1024], in_=gate[:, lo : lo + 1024])
 
-        pairs = held.tile([P, T, 2], BF16, name="pairs", align_bytes=64)
-        words = pairs[:].rearrange("p n e -> p (n e)").bitcast(U32)
-        plane2 = held.tile([P, T], BF16, name="plane2", align_bytes=64)
-        plane3 = held.tile([P, T], BF16, name="plane3", align_bytes=64)
-        mates = [
-            held.tile([P, 3 if c + EARLY < NCH else 2, CH, 2], BF16, name="mates" + str(c), align_bytes=64)
-            for c in range(EARLY)
-        ]
+        planes = [held.tile([P, T], BF16, name="plane" + str(j), align_bytes=64) for j in range(4)]
+        mates = [held.tile([P, 4, CH], BF16, name="mates" + str(c), align_bytes=64) for c in range(NCH)]
         result = held.tile([P, T], F32, name="result")
 
         def slots(c):
             return offsets[:, c * CH // 16 : (c + 1) * CH // 16]
 
-        def gather_words(c):
-            nc.vector.tensor_copy(
-                out=mates[c % EARLY][:, 0].rearrange("p n e -> p (n e)").bitcast(U32), in_=words.indirect(slots(c))
-            )
+        def cast(j):
+            for lo, hi, raw in raws[j]:
+                if j == 0:
+                    nc.vector.tensor_copy(out=planes[j][:, lo:hi], in_=raw[:])
+                else:
+                    cut = POOL_SHARE.get(hi, (hi - lo) // 2)
+                    nc.gpsimd.tensor_scalar(planes[j][:, lo : lo + cut], raw[:, :cut], 1.0, 0.0, MULT, ADD)
+                    if lo + cut < hi:
+                        nc.scalar.copy(out=planes[j][:, lo + cut : hi], in_=raw[:, cut:])
 
-        def gather_plane(plane, e, c):
-            nc.scalar.activation(mates[c % EARLY][:, 1 + c // EARLY, :, e], plane[:].indirect(slots(c)), COPY)
+        def gather(j, c, on_vector):
+            if on_vector:
+                nc.vector.tensor_copy(out=mates[c][:, j, :], in_=planes[j][:].indirect(slots(c)))
+            else:
+                nc.scalar.activation(mates[c][:, j, :], planes[j][:].indirect(slots(c)), COPY)
 
         laced = {}
         codes = {}
+        banks = {}
         squares = {}
 
         def lace(c):
             x4 = ring.tile([P, CH, 4], BF16, name="x4", align_bytes=64)
-            engine, word = (nc.vector.tensor_copy, I32) if c in V_LACE else (nc.scalar.copy, U32)
-            both = mates[c % EARLY][:].rearrange("p h n e -> p h (n e)").bitcast(word)
-            src = both[:, 0 : 2 + c // EARLY : 1 + c // EARLY, :].rearrange("p h n -> p n h")
-            dst = x4[:].rearrange("p n t -> p (n t)").bitcast(word).rearrange("p (n h) -> p n h", h=2)
-            engine(out=dst, in_=src)
+            engine = nc.vector.tensor_copy if c < V_LACE else nc.scalar.copy
+            engine(
+                out=x4[:].rearrange("p (c i) t -> p c t i", i=4),
+                in_=mates[c][:].rearrange("p t (c i) -> p c t i", i=4),
+            )
             laced[c] = x4
 
         def quantise(c):
@@ -148,11 +155,15 @@ def tile_moe_rag_lin_relu2_kernel(tc, xT, w_words, w_scales, b, gate, offs, out)
                     start=True,
                     stop=True,
                 )
+            banks[c] = bank
+
+        def activate(c):
             relu = ring.tile([N, CH], F32, name="relu")
-            for lo, hi, e in spans_of(c):
-                nc.scalar.activation(relu[:, lo:hi], bank[:, lo:hi], RELU, bias=b_sb[:, e : e + 1])
             square = ring.tile([N, CH], F32, name="square")
-            nc.scalar.activation(square[:], relu[:], SQUARE)
+            for lo, hi, e in spans_of(c):
+                nc.scalar.activation(relu[:, lo:hi], banks[c][:, lo:hi], RELU, bias=b_sb[:, e : e + 1])
+            for lo, hi, e in spans_of(c):
+                nc.scalar.activation(square[:, lo:hi], relu[:, lo:hi], SQUARE)
             squares[c] = square
 
         def scatter(c):
@@ -160,30 +171,20 @@ def tile_moe_rag_lin_relu2_kernel(tc, xT, w_words, w_scales, b, gate, offs, out)
                 result[:].indirect(slots(c)), squares[c][:], gate_sb[:, c * CH : (c + 1) * CH], MULT
             )
 
-        for lo, hi in zip(cuts2[:-1], cuts2[1:]):
-            nc.vector.tensor_copy(out=plane2[:, lo:hi], in_=raw2[:, lo:hi])
-        for c in range(NCH):
-            if c in V_PLANE:
-                nc.vector.tensor_copy(out=mates[c % EARLY][:, 1 + c // EARLY, :, 0], in_=raw2[:].indirect(slots(c)))
-            else:
-                gather_plane(plane2, 0, c)
-        for lo, hi, raw in raw01:
-            nc.vector.tensor_copy(out=pairs[:, lo:hi, :], in_=raw[:].rearrange("p e n -> p n e"))
-        for lo, hi, raw in raw3:
-            nc.scalar.copy(out=plane3[:, lo:hi], in_=raw[:, 0])
-        for c in range(EARLY):
-            gather_words(c)
+        cast(0)
+        for j in range(3):
+            for c in range(NCH):
+                gather(j, c, c >= V_FROM[j])
+            cast(j + 1)
 
-        for step in range(NCH + 3):
+        for step in range(NCH + 2):
             if step < NCH:
-                gather_plane(plane3, 1, step)
+                gather(3, step, step < V_LAST)
                 lace(step)
-            if 0 <= step - 1 < NCH:
-                quantise(step - 1)
-                multiply(step - 1)
-            if EARLY <= step - 1 + EARLY < NCH:
-                gather_words(step - 1 + EARLY)
-            if 0 <= step - 3 < NCH:
-                scatter(step - 3)
+                quantise(step)
+                multiply(step)
+            if step >= 2:
+                activate(step - 2)
+                scatter(step - 2)
         for queue, lo in ((nc.sync, 0), (nc.scalar, 2048)):
             queue.dma_start(out=out[:, lo : lo + 2048], in_=result[:, lo : lo + 2048])

@@ -47,11 +47,13 @@ def spans_of(c):
     return found
 
 
-V_FROM = (3, 3, 4)
-V_LACE = 4
+V_FROM = (1536, 1536, 2048)
+V_LACE = 3
 V_LAST = 1
+V_PART = 96
+REUSE = 3
 CUTS = (
-    (0, 2048, 3840, 4096),
+    (0, 2048, 3072, 3840, 4096),
     (0, 1024, 2048, 3072, 4096),
     (0, 1024, 2048, 3072, 4096),
     (0, 1024, 2048, 3072, 3840, 4096),
@@ -76,49 +78,55 @@ def tile_moe_rag_lin_relu2_kernel(tc, xT, w_words, w_scales, b, gate, offs, out)
 
         raws = []
         for j in range(4):
-            found = []
+            raw = held.tile([P, T], F32, name="raw" + str(j))
             for lo, hi in zip(CUTS[j][:-1], CUTS[j][1:]):
-                raw = held.tile([P, hi - lo], F32, name="raw" + str(j) + "_" + str(lo))
-                nc.sync.dma_start(out=raw[:], in_=rows[:, j, lo:hi])
-                found.append((lo, hi, raw))
+                nc.sync.dma_start(out=raw[:, lo:hi], in_=rows[:, j, lo:hi])
                 if j == 0 and lo == 0:
                     nc.sync.dma_start(offsets[:], offs)
-            raws.append(found)
+            raws.append(raw)
+            if j == 1:
+                for q in range(4):
+                    nc.sync.dma_start(
+                        out=ws_sb[32 * q : 32 * q + 4].bitcast(I32),
+                        in_=w_scales[:, 0, 4 * q : 4 * q + 4, :].rearrange("e q n -> q e n").bitcast(I32),
+                    )
+                nc.sync.dma_start(out=b_sb[:], in_=b)
         nc.sync.dma_start(
             out=w_sb[:].bitcast(I32), in_=w_words[:, 0].rearrange("e p n -> p e n").bitcast(I32)
         )
-        for q in range(4):
-            nc.sync.dma_start(
-                out=ws_sb[32 * q : 32 * q + 4].bitcast(I32),
-                in_=w_scales[:, 0, 4 * q : 4 * q + 4, :].rearrange("e q n -> q e n").bitcast(I32),
-            )
-        nc.sync.dma_start(out=b_sb[:], in_=b)
         gate_sb = held.tile([P, T], F32, name="gate_sb")
         for lo in range(0, T, 1024):
             nc.sync.dma_start(out=gate_sb[:, lo : lo + 1024], in_=gate[:, lo : lo + 1024])
 
         planes = [held.tile([P, T], BF16, name="plane" + str(j), align_bytes=64) for j in range(4)]
-        mates = [held.tile([P, 4, CH], BF16, name="mates" + str(c), align_bytes=64) for c in range(NCH)]
+        mates = {}
+        for first in range(REUSE):
+            chain = list(range(first, NCH, REUSE))
+            shared = held.tile([P, 3 * len(chain) + 1, CH], BF16, name="mates" + str(first), align_bytes=64)
+            for i, c in enumerate(reversed(chain)):
+                mates[c] = shared[:, 3 * i : 3 * i + 4, :]
         result = held.tile([P, T], F32, name="result")
 
-        def slots(c):
-            return offsets[:, c * CH // 16 : (c + 1) * CH // 16]
+        def slots(lo, hi):
+            return offsets[:, lo // 16 : hi // 16]
 
         def cast(j):
-            for lo, hi, raw in raws[j]:
+            for lo, hi in zip(CUTS[j][:-1], CUTS[j][1:]):
                 if j == 0:
-                    nc.vector.tensor_copy(out=planes[j][:, lo:hi], in_=raw[:])
+                    nc.vector.tensor_copy(out=planes[j][:, lo:hi], in_=raws[j][:, lo:hi])
                 else:
-                    cut = POOL_SHARE.get(hi, (hi - lo) // 2)
-                    nc.gpsimd.tensor_scalar(planes[j][:, lo : lo + cut], raw[:, :cut], 1.0, 0.0, MULT, ADD)
-                    if lo + cut < hi:
-                        nc.scalar.copy(out=planes[j][:, lo + cut : hi], in_=raw[:, cut:])
+                    cut = lo + POOL_SHARE.get(hi, (hi - lo) // 2)
+                    nc.gpsimd.tensor_scalar(planes[j][:, lo:cut], raws[j][:, lo:cut], 1.0, 0.0, MULT, ADD)
+                    if cut < hi:
+                        nc.scalar.copy(out=planes[j][:, cut:hi], in_=raws[j][:, cut:hi])
 
-        def gather(j, c, on_vector):
-            if on_vector:
-                nc.vector.tensor_copy(out=mates[c][:, j, :], in_=planes[j][:].indirect(slots(c)))
-            else:
-                nc.scalar.activation(mates[c][:, j, :], planes[j][:].indirect(slots(c)), COPY)
+        def gather_scalar(j, lo, hi):
+            c, at = divmod(lo, CH)
+            nc.scalar.activation(mates[c][:, j, at : at + hi - lo], planes[j][:].indirect(slots(lo, hi)), COPY)
+
+        def gather_vector(window, j, lo, hi):
+            c, at = divmod(lo, CH)
+            nc.vector.tensor_copy(out=mates[c][:, j, at : at + hi - lo], in_=window[:].indirect(slots(lo, hi)))
 
         laced = {}
         codes = {}
@@ -126,12 +134,14 @@ def tile_moe_rag_lin_relu2_kernel(tc, xT, w_words, w_scales, b, gate, offs, out)
         squares = {}
 
         def lace(c):
-            x4 = ring.tile([P, CH, 4], BF16, name="x4", align_bytes=64)
-            engine = nc.vector.tensor_copy if c < V_LACE else nc.scalar.copy
-            engine(
-                out=x4[:].rearrange("p (c i) t -> p c t i", i=4),
-                in_=mates[c][:].rearrange("p t (c i) -> p c t i", i=4),
-            )
+            x4 = ring.tile([P, CH, 4], BF16, name="x4", align_bytes=64, bufs=2)
+            cut = CH if c < V_LACE else V_PART
+            for engine, lo, hi in ((nc.vector.tensor_copy, 0, cut), (nc.scalar.copy, cut, CH)):
+                if lo < hi:
+                    engine(
+                        out=x4[:, lo:hi, :].rearrange("p (c i) t -> p c t i", i=4),
+                        in_=mates[c][:, :, lo:hi].rearrange("p t (c i) -> p c t i", i=4),
+                    )
             laced[c] = x4
 
         def quantise(c):
@@ -168,23 +178,32 @@ def tile_moe_rag_lin_relu2_kernel(tc, xT, w_words, w_scales, b, gate, offs, out)
 
         def scatter(c):
             nc.vector.tensor_tensor(
-                result[:].indirect(slots(c)), squares[c][:], gate_sb[:, c * CH : (c + 1) * CH], MULT
+                result[:].indirect(slots(c * CH, (c + 1) * CH)), squares[c][:], gate_sb[:, c * CH : (c + 1) * CH], MULT
             )
 
         cast(0)
         for j in range(3):
             for c in range(NCH):
-                gather(j, c, c >= V_FROM[j])
+                lo, hi = c * CH, (c + 1) * CH
+                cut = min(max(V_FROM[j], lo), hi)
+                if lo < cut:
+                    gather_scalar(j, lo, cut)
+                if cut < hi:
+                    gather_vector(planes[j], j, cut, hi)
             cast(j + 1)
 
         for step in range(NCH + 2):
             if step < NCH:
-                gather(3, step, step < V_LAST)
+                if step < V_LAST:
+                    gather_vector(raws[3], 3, step * CH, (step + 1) * CH)
+                else:
+                    gather_scalar(3, step * CH, (step + 1) * CH)
                 lace(step)
                 quantise(step)
                 multiply(step)
+            if 1 <= step <= NCH:
+                activate(step - 1)
             if step >= 2:
-                activate(step - 2)
                 scatter(step - 2)
         for queue, lo in ((nc.sync, 0), (nc.scalar, 2048)):
             queue.dma_start(out=out[:, lo : lo + 2048], in_=result[:, lo : lo + 2048])

@@ -48,10 +48,8 @@ def spans_of(c):
 
 
 V_FROM = (1536, 1536, 2048)
-V_LACE = 3
-V_LAST = 1
-V_PART = 96
-REUSE = 3
+V_LACE = 4
+REUSE = 4
 CUTS = (
     (0, 2048, 3072, 3840, 4096),
     (0, 1024, 2048, 3072, 4096),
@@ -84,16 +82,15 @@ def tile_moe_rag_lin_relu2_kernel(tc, xT, w_words, w_scales, b, gate, offs, out)
                 if j == 0 and lo == 0:
                     nc.sync.dma_start(offsets[:], offs)
             raws.append(raw)
-            if j == 1:
-                for q in range(4):
-                    nc.sync.dma_start(
-                        out=ws_sb[32 * q : 32 * q + 4].bitcast(I32),
-                        in_=w_scales[:, 0, 4 * q : 4 * q + 4, :].rearrange("e q n -> q e n").bitcast(I32),
-                    )
-                nc.sync.dma_start(out=b_sb[:], in_=b)
         nc.sync.dma_start(
             out=w_sb[:].bitcast(I32), in_=w_words[:, 0].rearrange("e p n -> p e n").bitcast(I32)
         )
+        for q in range(4):
+            nc.sync.dma_start(
+                out=ws_sb[32 * q : 32 * q + 4].bitcast(I32),
+                in_=w_scales[:, 0, 4 * q : 4 * q + 4, :].rearrange("e q n -> q e n").bitcast(I32),
+            )
+        nc.sync.dma_start(out=b_sb[:], in_=b)
         gate_sb = held.tile([P, T], F32, name="gate_sb")
         for lo in range(0, T, 1024):
             nc.sync.dma_start(out=gate_sb[:, lo : lo + 1024], in_=gate[:, lo : lo + 1024])
@@ -135,13 +132,11 @@ def tile_moe_rag_lin_relu2_kernel(tc, xT, w_words, w_scales, b, gate, offs, out)
 
         def lace(c):
             x4 = ring.tile([P, CH, 4], BF16, name="x4", align_bytes=64, bufs=2)
-            cut = CH if c < V_LACE else V_PART
-            for engine, lo, hi in ((nc.vector.tensor_copy, 0, cut), (nc.scalar.copy, cut, CH)):
-                if lo < hi:
-                    engine(
-                        out=x4[:, lo:hi, :].rearrange("p (c i) t -> p c t i", i=4),
-                        in_=mates[c][:, :, lo:hi].rearrange("p t (c i) -> p c t i", i=4),
-                    )
+            engine = nc.vector.tensor_copy if c < V_LACE else nc.scalar.copy
+            engine(
+                out=x4[:].rearrange("p (c i) t -> p c t i", i=4),
+                in_=mates[c].rearrange("p t (c i) -> p c t i", i=4),
+            )
             laced[c] = x4
 
         def quantise(c):
@@ -194,10 +189,7 @@ def tile_moe_rag_lin_relu2_kernel(tc, xT, w_words, w_scales, b, gate, offs, out)
 
         for step in range(NCH + 2):
             if step < NCH:
-                if step < V_LAST:
-                    gather_vector(raws[3], 3, step * CH, (step + 1) * CH)
-                else:
-                    gather_scalar(3, step * CH, (step + 1) * CH)
+                gather_scalar(3, step * CH, (step + 1) * CH)
                 lace(step)
                 quantise(step)
                 multiply(step)

@@ -47,16 +47,16 @@ def spans_of(c):
     return found
 
 
-V_FROM = (1536, 1536, 2048)
-V_LACE = 4
-REUSE = 4
-CUTS = (
-    (0, 2048, 3072, 3840, 4096),
-    (0, 1024, 2048, 3072, 4096),
-    (0, 1024, 2048, 3072, 4096),
-    (0, 1024, 2048, 3072, 3840, 4096),
-)
-POOL_SHARE = {1024: 1024, 2048: 1024, 3072: 640, 3840: 384}
+ORDER = (3, 0, 6, 7, 1, 2, 5, 4)
+CUTS2 = (0, 2048, 3584, 4096)
+CUTS01 = (0, 1792, 2816, 3456, 3840, 4096)
+CUTS3 = (0, 1024, 2048, 3072, 3840, 4096)
+POOL3 = (1024, 1024, 512, 384, 0)
+V_PLANE2 = 1
+V_LACES = (0, 1, 2)
+EARLY = 3840
+LAG = 2
+AHEAD = 4
 
 
 def tile_moe_rag_lin_relu2_kernel(tc, xT, w_words, w_scales, b, gate, offs, out):
@@ -64,7 +64,7 @@ def tile_moe_rag_lin_relu2_kernel(tc, xT, w_words, w_scales, b, gate, offs, out)
     with (
         tc.tile_pool(name="held", bufs=1) as held,
         tc.tile_pool(name="ring", bufs=3) as ring,
-        tc.psum_pool(name="psum", bufs=4) as psum,
+        tc.psum_pool(name="psum", bufs=5) as psum,
     ):
         offsets = held.tile([P, T // 16], U16, name="offsets")
         w_sb = held.tile([P, E, 2 * N], U8, name="w_sb", align_bytes=64)
@@ -74,77 +74,87 @@ def tile_moe_rag_lin_relu2_kernel(tc, xT, w_words, w_scales, b, gate, offs, out)
 
         rows = xT.rearrange("(p j) n -> p j n", j=4)
 
-        raws = []
-        for j in range(4):
+        def load_plane(j, cuts):
             raw = held.tile([P, T], F32, name="raw" + str(j))
-            for lo, hi in zip(CUTS[j][:-1], CUTS[j][1:]):
+            for lo, hi in zip(cuts[:-1], cuts[1:]):
                 nc.sync.dma_start(out=raw[:, lo:hi], in_=rows[:, j, lo:hi])
-                if j == 0 and lo == 0:
+                if j == 2 and lo == 0:
                     nc.sync.dma_start(offsets[:], offs)
-            raws.append(raw)
+            return raw
+
+        def load_small():
+            for q in range(4):
+                nc.sync.dma_start(
+                    out=ws_sb[32 * q : 32 * q + 4].bitcast(I32),
+                    in_=w_scales[:, 0, 4 * q : 4 * q + 4, :].rearrange("e q n -> q e n").bitcast(I32),
+                )
+            nc.sync.dma_start(out=b_sb[:], in_=b)
+
+        raw2 = load_plane(2, CUTS2)
+        raw01 = []
+        for lo, hi in zip(CUTS01[:-1], CUTS01[1:]):
+            piece = held.tile([P, 2, hi - lo], F32, name="raw01_" + str(lo))
+            nc.sync.dma_start(out=piece[:], in_=rows[:, 0:2, lo:hi])
+            raw01.append(piece)
+        raw3 = load_plane(3, CUTS3)
         nc.sync.dma_start(
             out=w_sb[:].bitcast(I32), in_=w_words[:, 0].rearrange("e p n -> p e n").bitcast(I32)
         )
-        for q in range(4):
-            nc.sync.dma_start(
-                out=ws_sb[32 * q : 32 * q + 4].bitcast(I32),
-                in_=w_scales[:, 0, 4 * q : 4 * q + 4, :].rearrange("e q n -> q e n").bitcast(I32),
-            )
-        nc.sync.dma_start(out=b_sb[:], in_=b)
+        load_small()
         gate_sb = held.tile([P, T], F32, name="gate_sb")
-        for lo in range(0, T, 1024):
+        for lo in (1024, 0, 3072, 2048):
             nc.sync.dma_start(out=gate_sb[:, lo : lo + 1024], in_=gate[:, lo : lo + 1024])
 
-        planes = [held.tile([P, T], BF16, name="plane" + str(j), align_bytes=64) for j in range(4)]
-        mates = {}
-        for first in range(REUSE):
-            chain = list(range(first, NCH, REUSE))
-            shared = held.tile([P, 3 * len(chain) + 1, CH], BF16, name="mates" + str(first), align_bytes=64)
-            for i, c in enumerate(reversed(chain)):
-                mates[c] = shared[:, 3 * i : 3 * i + 4, :]
+        plane2 = held.tile([P, T], BF16, name="plane2", align_bytes=64)
+        plane3 = held.tile([P, T], BF16, name="plane3", align_bytes=64)
+        pairs = held.tile([P, 2 * T], BF16, name="pairs", align_bytes=64)
+        mates = {c: held.tile([P, 4 * CH], BF16, name="mates" + str(c), align_bytes=64) for c in range(NCH)}
         result = held.tile([P, T], F32, name="result")
 
-        def slots(lo, hi):
-            return offsets[:, lo // 16 : hi // 16]
+        def slots(c):
+            return offsets[:, c * CH // 16 : (c + 1) * CH // 16]
 
-        def cast(j):
-            for lo, hi in zip(CUTS[j][:-1], CUTS[j][1:]):
-                if j == 0:
-                    nc.vector.tensor_copy(out=planes[j][:, lo:hi], in_=raws[j][:, lo:hi])
-                else:
-                    cut = lo + POOL_SHARE.get(hi, (hi - lo) // 2)
-                    nc.gpsimd.tensor_scalar(planes[j][:, lo:cut], raws[j][:, lo:cut], 1.0, 0.0, MULT, ADD)
-                    if cut < hi:
-                        nc.scalar.copy(out=planes[j][:, cut:hi], in_=raws[j][:, cut:hi])
+        def reach(c):
+            return EARLY if c == ORDER[0] else T
 
-        def gather_scalar(j, lo, hi):
-            c, at = divmod(lo, CH)
-            nc.scalar.activation(mates[c][:, j, at : at + hi - lo], planes[j][:].indirect(slots(lo, hi)), COPY)
+        def half(c, t):
+            return mates[c][:, 2 * CH :].rearrange("p (n t) -> p n t", t=2)[:, :, t]
 
-        def gather_vector(window, j, lo, hi):
-            c, at = divmod(lo, CH)
-            nc.vector.tensor_copy(out=mates[c][:, j, at : at + hi - lo], in_=window[:].indirect(slots(lo, hi)))
+        held_back = {ORDER[i]: ORDER[i + LAG] for i in range(AHEAD - LAG, NCH - LAG)}
+        for c in held_back.values():
+            nc.vector.memset(mates[c][:, 2 * CH : 2 * CH + 2], 0.0)
 
+        def gather_words(c):
+            nc.vector.tensor_copy(
+                out=mates[c][:, : 2 * CH].bitcast(U32), in_=pairs[:, : 2 * reach(c)].bitcast(U32).indirect(slots(c))
+            )
+
+        def gather_last(c):
+            nc.scalar.activation(half(c, 1), plane3[:, : reach(c)].indirect(slots(c)), COPY)
+
+        late = held.tile([P, 4 * CH], BF16, name="late", align_bytes=64)
         laced = {}
         codes = {}
         banks = {}
         squares = {}
 
         def lace(c):
-            x4 = ring.tile([P, CH, 4], BF16, name="x4", align_bytes=64, bufs=2)
-            engine = nc.vector.tensor_copy if c < V_LACE else nc.scalar.copy
+            if c == ORDER[AHEAD - 1]:
+                x4 = late
+            else:
+                x4 = ring.tile([P, 4 * CH], BF16, name="x4", align_bytes=64, bufs=3)
+            on_vector = ORDER.index(c) in V_LACES
+            engine, word = (nc.vector.tensor_copy, I32) if on_vector else (nc.scalar.copy, U32)
             engine(
-                out=x4[:].rearrange("p (c i) t -> p c t i", i=4),
-                in_=mates[c].rearrange("p t (c i) -> p c t i", i=4),
+                out=x4[:].bitcast(word).rearrange("p (n u) -> p n u", u=2),
+                in_=mates[c][:].bitcast(word).rearrange("p (u n) -> p n u", u=2),
             )
             laced[c] = x4
 
         def quantise(c):
             cw = ring.tile([P, CH], U32, name="cw", align_bytes=64)
             cs = ring.tile([P, CH], U8, name="cs", align_bytes=64)
-            nc.vector.quantize_mx(
-                out=cw[:].bitcast(FP8X4), scales=cs[:], in_=laced[c][:].rearrange("p n t -> p (n t)")
-            )
+            nc.vector.quantize_mx(out=cw[:].bitcast(FP8X4), scales=cs[:], in_=laced[c][:])
             codes[c] = (cw, cs)
 
         def multiply(c):
@@ -163,39 +173,75 @@ def tile_moe_rag_lin_relu2_kernel(tc, xT, w_words, w_scales, b, gate, offs, out)
             banks[c] = bank
 
         def activate(c):
-            relu = ring.tile([N, CH], F32, name="relu")
-            square = ring.tile([N, CH], F32, name="square")
+            if c == ORDER[0]:
+                relu = late[:, : 2 * CH].bitcast(F32)
+            else:
+                relu = ring.tile([N, CH], F32, name="relu")[:]
+            place = ORDER.index(c) + 1
+            if AHEAD - 1 <= place < NCH and place not in V_LACES:
+                square = mates[ORDER[place]][:, : 2 * CH].bitcast(F32)
+            else:
+                square = ring.tile([N, CH], F32, name="square")[:]
             for lo, hi, e in spans_of(c):
                 nc.scalar.activation(relu[:, lo:hi], banks[c][:, lo:hi], RELU, bias=b_sb[:, e : e + 1])
-            for lo, hi, e in spans_of(c):
-                nc.scalar.activation(square[:, lo:hi], relu[:, lo:hi], SQUARE)
+            for n, (lo, hi, e) in enumerate(spans_of(c)):
+                if n == 0 and c in held_back:
+                    nc.scalar.activation(square[:, lo:hi], relu[:, lo:hi], SQUARE, bias=half(held_back[c], 1)[:, 0:1])
+                else:
+                    nc.scalar.activation(square[:, lo:hi], relu[:, lo:hi], SQUARE)
             squares[c] = square
 
         def scatter(c):
             nc.vector.tensor_tensor(
-                result[:].indirect(slots(c * CH, (c + 1) * CH)), squares[c][:], gate_sb[:, c * CH : (c + 1) * CH], MULT
+                result[:].indirect(slots(c)), squares[c], gate_sb[:, c * CH : (c + 1) * CH], MULT
             )
 
-        cast(0)
-        for j in range(3):
-            for c in range(NCH):
-                lo, hi = c * CH, (c + 1) * CH
-                cut = min(max(V_FROM[j], lo), hi)
-                if lo < cut:
-                    gather_scalar(j, lo, cut)
-                if cut < hi:
-                    gather_vector(planes[j], j, cut, hi)
-            cast(j + 1)
+        for lo, hi in zip(CUTS2[:-1], CUTS2[1:]):
+            nc.vector.tensor_copy(out=plane2[:, lo:hi], in_=raw2[:, lo:hi])
+        for i, c in enumerate(ORDER):
+            if i < NCH - V_PLANE2:
+                nc.scalar.activation(half(c, 0), plane2[:].indirect(slots(c)), COPY)
+            else:
+                nc.vector.tensor_copy(out=half(c, 0), in_=raw2[:].indirect(slots(c)))
+        for lo, hi, piece in zip(CUTS01[:-1], CUTS01[1:], raw01):
+            laid = pairs[:, 2 * lo : 2 * hi].rearrange("p (n j) -> p n j", j=2)
+            if lo < EARLY:
+                nc.vector.tensor_copy(out=laid, in_=piece[:].rearrange("p j n -> p n j"))
+            else:
+                nc.gpsimd.tensor_scalar(laid, piece[:].rearrange("p j n -> p n j"), 1.0, 0.0, MULT, ADD)
+        for c in ORDER:
+            gather_words(c)
+        for lo, hi, share in zip(CUTS3[:-1], CUTS3[1:], POOL3):
+            if lo == EARLY:
+                gather_last(ORDER[0])
+            cut = lo + share
+            if lo < cut:
+                nc.gpsimd.tensor_scalar(plane3[:, lo:cut], raw3[:, lo:cut], 1.0, 0.0, MULT, ADD)
+            if cut < hi:
+                nc.scalar.copy(out=plane3[:, cut:hi], in_=raw3[:, cut:hi])
 
-        for step in range(NCH + 2):
-            if step < NCH:
-                gather_scalar(3, step * CH, (step + 1) * CH)
-                lace(step)
-                quantise(step)
-                multiply(step)
-            if 1 <= step <= NCH:
-                activate(step - 1)
-            if step >= 2:
-                scatter(step - 2)
+        def front(i):
+            lace(ORDER[i])
+            quantise(ORDER[i])
+            multiply(ORDER[i])
+
+        def back(i):
+            activate(ORDER[i])
+            scatter(ORDER[i])
+
+        for i in range(AHEAD):
+            if i > 0:
+                gather_last(ORDER[i])
+            if i < AHEAD - 1:
+                front(i)
+        back(0)
+        back(1)
+        front(AHEAD - 1)
+        for i in range(AHEAD, NCH):
+            back(i - LAG)
+            gather_last(ORDER[i])
+            front(i)
+        back(NCH - 2)
+        back(NCH - 1)
         for queue, lo in ((nc.sync, 0), (nc.scalar, 2048)):
             queue.dma_start(out=out[:, lo : lo + 2048], in_=result[:, lo : lo + 2048])

@@ -36,26 +36,25 @@ def pieces_of(c):
 
 def spans_of(c):
     found = []
-    start = 0
-    for e in range(E):
-        lo, hi = max(start, c * CH), min(start + COUNTS[e], (c + 1) * CH)
-        start += COUNTS[e]
-        if hi - lo == CH:
-            found.extend([(0, CH // 2, e), (CH // 2, CH, e)])
-        elif lo < hi:
-            found.append((lo - c * CH, hi - c * CH, e))
+    for half_start in (c * CH, c * CH + CH // 2):
+        start = 0
+        for e in range(E):
+            lo, hi = max(start, half_start), min(start + COUNTS[e], half_start + CH // 2)
+            start += COUNTS[e]
+            if lo < hi:
+                found.append((lo - c * CH, hi - c * CH, e))
     return found
 
 
 ORDER = (3, 0, 6, 7, 1, 2, 5, 4)
-CUTS2 = (0, 2048, 3584, 4096)
-CUTS01 = (0, 1792, 2816, 3456, 3840, 4096)
-CUTS3 = (0, 1024, 2048, 3072, 3840, 4096)
-POOL3 = (1024, 1024, 512, 384, 0)
-V_PLANE2 = 1
-V_LACES = (0, 1, 2)
+CUTS2 = (0, 2560, 4096)
+CUTS01 = (0, 2048, 3200, 3840, 4096)
+CUTS3 = (0, 1280, 2560, 3328, 3840, 4096)
+POOL3 = (1280, 640, 384, 256, 256)
+V_PLANE2 = 2
+V_LACES = (0, 1, 2, 3)
 EARLY = 3840
-LAG = 2
+LAG = 3
 AHEAD = 4
 
 
@@ -132,18 +131,18 @@ def tile_moe_rag_lin_relu2_kernel(tc, xT, w_words, w_scales, b, gate, offs, out)
         def gather_last(c):
             nc.scalar.activation(half(c, 1), plane3[:, : reach(c)].indirect(slots(c)), COPY)
 
-        late = held.tile([P, 4 * CH], BF16, name="late", align_bytes=64)
+        late = {c: held.tile([P, 4 * CH], BF16, name="late" + str(c), align_bytes=64) for c in ORDER[AHEAD:]}
         laced = {}
         codes = {}
         banks = {}
         squares = {}
 
         def lace(c):
-            if c == ORDER[AHEAD - 1]:
-                x4 = late
-            else:
-                x4 = ring.tile([P, 4 * CH], BF16, name="x4", align_bytes=64, bufs=3)
             on_vector = ORDER.index(c) in V_LACES
+            if on_vector:
+                x4 = ring.tile([P, 4 * CH], BF16, name="x4", align_bytes=64, bufs=3)
+            else:
+                x4 = late[c]
             engine, word = (nc.vector.tensor_copy, I32) if on_vector else (nc.scalar.copy, U32)
             engine(
                 out=x4[:].bitcast(word).rearrange("p (n u) -> p n u", u=2),
@@ -173,18 +172,18 @@ def tile_moe_rag_lin_relu2_kernel(tc, xT, w_words, w_scales, b, gate, offs, out)
             banks[c] = bank
 
         def activate(c):
-            if c == ORDER[0]:
-                relu = late[:, : 2 * CH].bitcast(F32)
+            if AHEAD <= ORDER.index(c) + 2 < NCH:
+                relu = late[ORDER[ORDER.index(c) + 2]][:, : 2 * CH].bitcast(F32)
             else:
                 relu = ring.tile([N, CH], F32, name="relu")[:]
             place = ORDER.index(c) + 1
-            if AHEAD - 1 <= place < NCH and place not in V_LACES:
+            if AHEAD <= place < NCH and place not in V_LACES:
                 square = mates[ORDER[place]][:, : 2 * CH].bitcast(F32)
             else:
                 square = ring.tile([N, CH], F32, name="square")[:]
             for lo, hi, e in spans_of(c):
                 nc.scalar.activation(relu[:, lo:hi], banks[c][:, lo:hi], RELU, bias=b_sb[:, e : e + 1])
-            for n, (lo, hi, e) in enumerate(spans_of(c)):
+            for n, (lo, hi) in enumerate(((0, CH // 2), (CH // 2, CH))):
                 if n == 0 and c in held_back:
                     nc.scalar.activation(square[:, lo:hi], relu[:, lo:hi], SQUARE, bias=half(held_back[c], 1)[:, 0:1])
                 else:
@@ -232,16 +231,12 @@ def tile_moe_rag_lin_relu2_kernel(tc, xT, w_words, w_scales, b, gate, offs, out)
         for i in range(AHEAD):
             if i > 0:
                 gather_last(ORDER[i])
-            if i < AHEAD - 1:
-                front(i)
-        back(0)
-        back(1)
-        front(AHEAD - 1)
-        for i in range(AHEAD, NCH):
-            back(i - LAG)
-            gather_last(ORDER[i])
             front(i)
-        back(NCH - 2)
-        back(NCH - 1)
+        for i in range(NCH):
+            back(i)
+            if AHEAD <= i + 2 < NCH:
+                front(i + 2)
+            if AHEAD <= i + LAG < NCH:
+                gather_last(ORDER[i + LAG])
         for queue, lo in ((nc.sync, 0), (nc.scalar, 2048)):
             queue.dma_start(out=out[:, lo : lo + 2048], in_=result[:, lo : lo + 2048])

@@ -46,12 +46,12 @@ def spans_of(c):
     return found
 
 
-ORDER = (3, 0, 6, 7, 1, 2, 5, 4)
+ORDER = (3, 6, 7, 0, 1, 2, 4, 5)
 CUTS2 = (0, 2560, 4096)
-CUTS01 = (0, 2048, 3200, 3840, 4096)
+CUTS01 = (0, 1024, 2304, 3200, 3584, 3840, 4096)
 CUTS3 = (0, 1280, 2560, 3328, 3840, 4096)
 POOL3 = (1280, 640, 384, 256, 256)
-V_PLANE2 = 2
+RUNS = ((3, 1), (6, 2), (0, 3), (4, 2))
 V_LACES = (0, 1, 2, 3)
 EARLY = 3840
 LAG = 3
@@ -101,37 +101,46 @@ def tile_moe_rag_lin_relu2_kernel(tc, xT, w_words, w_scales, b, gate, offs, out)
         )
         load_small()
         gate_sb = held.tile([P, T], F32, name="gate_sb")
-        for lo in (1024, 0, 3072, 2048):
+        for lo in (1024, 3072, 0, 2048):
             nc.sync.dma_start(out=gate_sb[:, lo : lo + 1024], in_=gate[:, lo : lo + 1024])
 
         plane2 = held.tile([P, T], BF16, name="plane2", align_bytes=64)
         plane3 = held.tile([P, T], BF16, name="plane3", align_bytes=64)
         pairs = held.tile([P, 2 * T], BF16, name="pairs", align_bytes=64)
-        mates = {c: held.tile([P, 4 * CH], BF16, name="mates" + str(c), align_bytes=64) for c in range(NCH)}
+        mates = held.tile([P, 4 * T], BF16, name="mates", align_bytes=64)
         result = held.tile([P, T], F32, name="result")
 
-        def slots(c):
-            return offsets[:, c * CH // 16 : (c + 1) * CH // 16]
+        def slots(c, count=1):
+            return offsets[:, c * CH // 16 : (c + count) * CH // 16]
+
+        def low(c, count=1):
+            at = ORDER.index(c) * 2 * CH
+            return mates[:, at : at + count * 2 * CH]
+
+        def high(c, count=1):
+            at = 2 * T + ORDER.index(c) * 2 * CH
+            return mates[:, at : at + count * 2 * CH]
 
         def reach(c):
             return EARLY if c == ORDER[0] else T
 
-        def half(c, t):
-            return mates[c][:, 2 * CH :].rearrange("p (n t) -> p n t", t=2)[:, :, t]
+        def half(c, t, count=1):
+            return high(c, count).rearrange("p (n t) -> p n t", t=2)[:, :, t]
 
         held_back = {ORDER[i]: ORDER[i + LAG] for i in range(AHEAD - LAG, NCH - LAG)}
         for c in held_back.values():
-            nc.vector.memset(mates[c][:, 2 * CH : 2 * CH + 2], 0.0)
+            nc.vector.memset(high(c)[:, 0:2], 0.0)
 
-        def gather_words(c):
+        def gather_words(c, count):
             nc.vector.tensor_copy(
-                out=mates[c][:, : 2 * CH].bitcast(U32), in_=pairs[:, : 2 * reach(c)].bitcast(U32).indirect(slots(c))
+                out=low(c, count).bitcast(U32), in_=pairs[:, : 2 * reach(c)].bitcast(U32).indirect(slots(c, count))
             )
 
         def gather_last(c):
             nc.scalar.activation(half(c, 1), plane3[:, : reach(c)].indirect(slots(c)), COPY)
 
         late = {c: held.tile([P, 4 * CH], BF16, name="late" + str(c), align_bytes=64) for c in ORDER[AHEAD:]}
+        both = held.tile([N, 2 * CH], F32, name="both")
         laced = {}
         codes = {}
         banks = {}
@@ -139,6 +148,7 @@ def tile_moe_rag_lin_relu2_kernel(tc, xT, w_words, w_scales, b, gate, offs, out)
 
         def lace(c):
             on_vector = ORDER.index(c) in V_LACES
+            at = ORDER.index(c) * CH
             if on_vector:
                 x4 = ring.tile([P, 4 * CH], BF16, name="x4", align_bytes=64, bufs=3)
             else:
@@ -146,7 +156,7 @@ def tile_moe_rag_lin_relu2_kernel(tc, xT, w_words, w_scales, b, gate, offs, out)
             engine, word = (nc.vector.tensor_copy, I32) if on_vector else (nc.scalar.copy, U32)
             engine(
                 out=x4[:].bitcast(word).rearrange("p (n u) -> p n u", u=2),
-                in_=mates[c][:].bitcast(word).rearrange("p (u n) -> p n u", u=2),
+                in_=mates[:].bitcast(word).rearrange("p (u n) -> p n u", u=2)[:, at : at + CH, :],
             )
             laced[c] = x4
 
@@ -178,7 +188,9 @@ def tile_moe_rag_lin_relu2_kernel(tc, xT, w_words, w_scales, b, gate, offs, out)
                 relu = ring.tile([N, CH], F32, name="relu")[:]
             place = ORDER.index(c) + 1
             if AHEAD <= place < NCH and place not in V_LACES:
-                square = mates[ORDER[place]][:, : 2 * CH].bitcast(F32)
+                square = low(ORDER[place]).bitcast(F32)
+            elif place - 1 in (1, 2):
+                square = both[:, (place - 2) * CH : (place - 1) * CH]
             else:
                 square = ring.tile([N, CH], F32, name="square")[:]
             for lo, hi, e in spans_of(c):
@@ -197,19 +209,18 @@ def tile_moe_rag_lin_relu2_kernel(tc, xT, w_words, w_scales, b, gate, offs, out)
 
         for lo, hi in zip(CUTS2[:-1], CUTS2[1:]):
             nc.vector.tensor_copy(out=plane2[:, lo:hi], in_=raw2[:, lo:hi])
-        for i, c in enumerate(ORDER):
-            if i < NCH - V_PLANE2:
-                nc.scalar.activation(half(c, 0), plane2[:].indirect(slots(c)), COPY)
-            else:
-                nc.vector.tensor_copy(out=half(c, 0), in_=raw2[:].indirect(slots(c)))
+        for c, count in RUNS[:-1]:
+            nc.scalar.activation(half(c, 0, count), plane2[:].indirect(slots(c, count)), COPY)
+        c, count = RUNS[-1]
+        nc.vector.tensor_copy(out=half(c, 0, count), in_=raw2[:].indirect(slots(c, count)))
         for lo, hi, piece in zip(CUTS01[:-1], CUTS01[1:], raw01):
             laid = pairs[:, 2 * lo : 2 * hi].rearrange("p (n j) -> p n j", j=2)
-            if lo < EARLY:
+            if 0 < lo < EARLY:
                 nc.vector.tensor_copy(out=laid, in_=piece[:].rearrange("p j n -> p n j"))
             else:
                 nc.gpsimd.tensor_scalar(laid, piece[:].rearrange("p j n -> p n j"), 1.0, 0.0, MULT, ADD)
-        for c in ORDER:
-            gather_words(c)
+        for c, count in RUNS:
+            gather_words(c, count)
         for lo, hi, share in zip(CUTS3[:-1], CUTS3[1:], POOL3):
             if lo == EARLY:
                 gather_last(ORDER[0])
@@ -232,11 +243,18 @@ def tile_moe_rag_lin_relu2_kernel(tc, xT, w_words, w_scales, b, gate, offs, out)
             if i > 0:
                 gather_last(ORDER[i])
             front(i)
-        for i in range(NCH):
-            back(i)
-            if AHEAD <= i + 2 < NCH:
+        back(0)
+        activate(ORDER[1])
+        activate(ORDER[2])
+        c = ORDER[1]
+        nc.vector.tensor_tensor(result[:].indirect(slots(c, 2)), both[:], gate_sb[:, c * CH : (c + 2) * CH], MULT)
+        gather_last(ORDER[AHEAD])
+        for i in range(2, NCH):
+            if i > 2:
+                back(i)
+            if i + 2 < NCH:
                 front(i + 2)
-            if AHEAD <= i + LAG < NCH:
+            if i + LAG < NCH:
                 gather_last(ORDER[i + LAG])
         for queue, lo in ((nc.sync, 0), (nc.scalar, 2048)):
             queue.dma_start(out=out[:, lo : lo + 2048], in_=result[:, lo : lo + 2048])

@@ -127,7 +127,7 @@ def tile_moe_rag_lin_relu2_kernel(tc, xT, w_words, w_scales, b, gate, offs, out)
         def half(c, t, count=1):
             return high(c, count).rearrange("p (n t) -> p n t", t=2)[:, :, t]
 
-        held_back = {ORDER[i]: ORDER[i + LAG] for i in range(AHEAD - LAG, NCH - LAG)}
+        held_back = {(ORDER[2], 0): ORDER[4], (ORDER[2], 1): ORDER[5], (ORDER[3], 0): ORDER[6], (ORDER[4], 0): ORDER[7]}
         for c in held_back.values():
             nc.vector.memset(high(c)[:, 0:2], 0.0)
 
@@ -141,6 +141,9 @@ def tile_moe_rag_lin_relu2_kernel(tc, xT, w_words, w_scales, b, gate, offs, out)
 
         late = {c: held.tile([P, 4 * CH], BF16, name="late" + str(c), align_bytes=64) for c in ORDER[AHEAD:]}
         both = held.tile([N, 2 * CH], F32, name="both")
+        relu = held.tile([N, CH], F32, name="relu")
+        for c in ORDER[AHEAD:]:
+            nc.vector.memset(late[c][:, 0:2].bitcast(F32), 1.0)
         laced = {}
         codes = {}
         banks = {}
@@ -182,10 +185,6 @@ def tile_moe_rag_lin_relu2_kernel(tc, xT, w_words, w_scales, b, gate, offs, out)
             banks[c] = bank
 
         def activate(c):
-            if AHEAD <= ORDER.index(c) + 2 < NCH:
-                relu = late[ORDER[ORDER.index(c) + 2]][:, : 2 * CH].bitcast(F32)
-            else:
-                relu = ring.tile([N, CH], F32, name="relu")[:]
             place = ORDER.index(c) + 1
             if AHEAD <= place < NCH and place not in V_LACES:
                 square = low(ORDER[place]).bitcast(F32)
@@ -196,10 +195,9 @@ def tile_moe_rag_lin_relu2_kernel(tc, xT, w_words, w_scales, b, gate, offs, out)
             for lo, hi, e in spans_of(c):
                 nc.scalar.activation(relu[:, lo:hi], banks[c][:, lo:hi], RELU, bias=b_sb[:, e : e + 1])
             for n, (lo, hi) in enumerate(((0, CH // 2), (CH // 2, CH))):
-                if n == 0 and c in held_back:
-                    nc.scalar.activation(square[:, lo:hi], relu[:, lo:hi], SQUARE, bias=half(held_back[c], 1)[:, 0:1])
-                else:
-                    nc.scalar.activation(square[:, lo:hi], relu[:, lo:hi], SQUARE)
+                zero = half(held_back[c, n], 1)[:, 0:1] if (c, n) in held_back else 0.0
+                one = late[ORDER[place + 1]][:, 0:2].bitcast(F32) if n == 1 and AHEAD <= place + 1 < NCH else 1.0
+                nc.scalar.activation(square[:, lo:hi], relu[:, lo:hi], SQUARE, bias=zero, scale=one)
             squares[c] = square
 
         def scatter(c):
@@ -252,9 +250,9 @@ def tile_moe_rag_lin_relu2_kernel(tc, xT, w_words, w_scales, b, gate, offs, out)
         for i in range(2, NCH):
             if i > 2:
                 back(i)
-            if i + 2 < NCH:
-                front(i + 2)
             if i + LAG < NCH:
                 gather_last(ORDER[i + LAG])
+            if i + 2 < NCH:
+                front(i + 2)
         for queue, lo in ((nc.sync, 0), (nc.scalar, 2048)):
             queue.dma_start(out=out[:, lo : lo + 2048], in_=result[:, lo : lo + 2048])

@@ -127,7 +127,7 @@ def tile_moe_rag_lin_relu2_kernel(tc, xT, w_words, w_scales, b, gate, offs, out)
         def half(c, t, count=1):
             return high(c, count).rearrange("p (n t) -> p n t", t=2)[:, :, t]
 
-        held_back = {(ORDER[2], 0): ORDER[4], (ORDER[2], 1): ORDER[5], (ORDER[3], 0): ORDER[6], (ORDER[4], 0): ORDER[7]}
+        held_back = {(ORDER[2], 0): ORDER[4], (ORDER[2], 1): ORDER[5], (ORDER[3], 0): ORDER[6], (ORDER[5], 0): ORDER[7]}
         for c in held_back.values():
             nc.vector.memset(high(c)[:, 0:2], 0.0)
 
@@ -196,7 +196,7 @@ def tile_moe_rag_lin_relu2_kernel(tc, xT, w_words, w_scales, b, gate, offs, out)
                 nc.scalar.activation(relu[:, lo:hi], banks[c][:, lo:hi], RELU, bias=b_sb[:, e : e + 1])
             for n, (lo, hi) in enumerate(((0, CH // 2), (CH // 2, CH))):
                 zero = half(held_back[c, n], 1)[:, 0:1] if (c, n) in held_back else 0.0
-                one = late[ORDER[place + 1]][:, 0:2].bitcast(F32) if n == 1 and AHEAD <= place + 1 < NCH else 1.0
+                one = late[ORDER[place + 1]][:, 0:2].bitcast(F32) if n == 0 and AHEAD <= place + 1 < NCH else 1.0
                 nc.scalar.activation(square[:, lo:hi], relu[:, lo:hi], SQUARE, bias=zero, scale=one)
             squares[c] = square
 
@@ -250,8 +250,8 @@ def tile_moe_rag_lin_relu2_kernel(tc, xT, w_words, w_scales, b, gate, offs, out)
         for i in range(2, NCH):
             if i > 2:
                 back(i)
-            if i + LAG < NCH:
-                gather_last(ORDER[i + LAG])
+            if i != 4 and i + 2 < NCH:
+                gather_last(ORDER[min(i + LAG, NCH - 1)])
             if i + 2 < NCH:
                 front(i + 2)
         for queue, lo in ((nc.sync, 0), (nc.scalar, 2048)):

@@ -12,21 +12,31 @@ RELU = mybir.ActivationFunctionType.Relu
 COPY = mybir.ActivationFunctionType.Copy
 SQUARE = mybir.ActivationFunctionType.Square
 MULT = mybir.AluOpType.mult
-ADD = mybir.AluOpType.add
 
 P, T, E, N, K = 128, 4096, 8, 128, 512
 COUNTS = (128, 128, 512, 640, 896, 896, 384, 512)
 FLOPS = 2 * K * N * T
 CH = 512
 NCH = T // CH
+HALF = NCH // 2
+RUN = 4
+SHIFT = 256
+
+
+def expert_spans(lo, hi):
+    found = []
+    start = 0
+    for e in range(E):
+        a, z = max(start, lo), min(start + COUNTS[e], hi)
+        start += COUNTS[e]
+        if a < z:
+            found.append((a, z, e))
+    return found
 
 
 def pieces_of(c):
     found = []
-    start = 0
-    for e in range(E):
-        lo, hi = max(start, c * CH), min(start + COUNTS[e], (c + 1) * CH)
-        start += COUNTS[e]
+    for lo, hi, e in expert_spans(c * CH, (c + 1) * CH):
         while lo < hi:
             width = max(n for n in (128, 256, 512) if n <= hi - lo)
             found.append((lo - c * CH, width, e))
@@ -34,143 +44,97 @@ def pieces_of(c):
     return found
 
 
-def spans_of(c):
-    found = []
-    for half_start in (c * CH, c * CH + CH // 2):
-        start = 0
-        for e in range(E):
-            lo, hi = max(start, half_start), min(start + COUNTS[e], half_start + CH // 2)
-            start += COUNTS[e]
-            if lo < hi:
-                found.append((lo - c * CH, hi - c * CH, e))
-    return found
-
-
-ORDER = (3, 6, 7, 0, 1, 2, 4, 5)
-CUTS2 = (0, 2560, 4096)
-CUTS01 = (0, 1024, 2304, 3200, 3584, 3840, 4096)
-CUTS3 = (0, 1280, 2560, 3328, 3840, 4096)
-POOL3 = (1280, 640, 384, 256, 256)
-RUNS = ((3, 1), (6, 2), (0, 3), (4, 2))
-V_LACES = (0, 1, 2, 3)
-EARLY = 3840
-LAG = 3
-AHEAD = 4
-
-
 def tile_moe_rag_lin_relu2_kernel(tc, xT, w_words, w_scales, b, gate, offs, out):
     nc = tc.nc
     with (
         tc.tile_pool(name="held", bufs=1) as held,
-        tc.tile_pool(name="ring", bufs=3) as ring,
-        tc.psum_pool(name="psum", bufs=5) as psum,
+        tc.tile_pool(name="ring", bufs=NCH) as ring,
+        tc.psum_pool(name="psum", bufs=NCH) as psum,
     ):
         offsets = held.tile([P, T // 16], U16, name="offsets")
         w_sb = held.tile([P, E, 2 * N], U8, name="w_sb", align_bytes=64)
         ws_sb = held.tile([P, E, N], U8, name="ws_sb", align_bytes=64)
         b_sb = held.tile([P, E], F32, name="b_sb")
+        gate_sb = held.tile([P, T], F32, name="gate_sb")
         nc.vector.memset(ws_sb[:].rearrange("p e n -> p (e n)").bitcast(I32), 0)
 
+        warm = held.tile([P, 2], F32, name="warm")
+        nc.vector.memset(warm[:, 0:1], 0.0)
+        nc.scalar.activation(warm[:, 1:2], warm[:, 0:1], SQUARE)
+
         rows = xT.rearrange("(p j) n -> p j n", j=4)
+        raw = []
+        for j in range(4):
+            plane = held.tile([P, T], F32, name="raw" + str(j))
+            nc.sync.dma_start(out=plane[:], in_=rows[:, j, :])
+            if j == 0:
+                nc.sync.dma_start(offsets[:], offs)
+            raw.append(plane)
+        nc.sync.dma_start(out=w_sb[:].bitcast(I32), in_=w_words[:, 0].rearrange("e p n -> p e n").bitcast(I32))
+        for q in range(4):
+            nc.sync.dma_start(
+                out=ws_sb[32 * q : 32 * q + 4].bitcast(I32),
+                in_=w_scales[:, 0, 4 * q : 4 * q + 4, :].rearrange("e q n -> q e n").bitcast(I32),
+            )
+        nc.sync.dma_start(out=b_sb[:], in_=b)
+        for lo in range(0, T, 2 * CH):
+            nc.sync.dma_start(out=gate_sb[:, lo : lo + 2 * CH], in_=gate[:, lo : lo + 2 * CH])
 
-        def load_plane(j, cuts):
-            raw = held.tile([P, T], F32, name="raw" + str(j))
-            for lo, hi in zip(cuts[:-1], cuts[1:]):
-                nc.sync.dma_start(out=raw[:, lo:hi], in_=rows[:, j, lo:hi])
-                if j == 2 and lo == 0:
-                    nc.sync.dma_start(offsets[:], offs)
-            return raw
-
-        def load_small():
-            for q in range(4):
-                nc.sync.dma_start(
-                    out=ws_sb[32 * q : 32 * q + 4].bitcast(I32),
-                    in_=w_scales[:, 0, 4 * q : 4 * q + 4, :].rearrange("e q n -> q e n").bitcast(I32),
-                )
-            nc.sync.dma_start(out=b_sb[:], in_=b)
-
-        raw2 = load_plane(2, CUTS2)
-        raw01 = []
-        for lo, hi in zip(CUTS01[:-1], CUTS01[1:]):
-            piece = held.tile([P, 2, hi - lo], F32, name="raw01_" + str(lo))
-            nc.sync.dma_start(out=piece[:], in_=rows[:, 0:2, lo:hi])
-            raw01.append(piece)
-        raw3 = load_plane(3, CUTS3)
-        nc.sync.dma_start(
-            out=w_sb[:].bitcast(I32), in_=w_words[:, 0].rearrange("e p n -> p e n").bitcast(I32)
-        )
-        load_small()
-        gate_sb = held.tile([P, T], F32, name="gate_sb")
-        for lo in (1024, 3072, 0, 2048):
-            nc.sync.dma_start(out=gate_sb[:, lo : lo + 1024], in_=gate[:, lo : lo + 1024])
-
-        plane2 = held.tile([P, T], BF16, name="plane2", align_bytes=64)
-        plane3 = held.tile([P, T], BF16, name="plane3", align_bytes=64)
-        pairs = held.tile([P, 2 * T], BF16, name="pairs", align_bytes=64)
-        mates = held.tile([P, 4 * T], BF16, name="mates", align_bytes=64)
+        early = held.tile([P, 4 * HALF * CH], BF16, name="early", align_bytes=64)
+        late = held.tile([P, (HALF + 1) * 4 * CH], BF16, name="late", align_bytes=64)
+        spare = held.tile([P, CH], F32, name="spare")
+        squares = held.tile([N, T], F32, name="squares")
         result = held.tile([P, T], F32, name="result")
 
         def slots(c, count=1):
             return offsets[:, c * CH // 16 : (c + count) * CH // 16]
 
-        def low(c, count=1):
-            at = ORDER.index(c) * 2 * CH
-            return mates[:, at : at + count * 2 * CH]
+        def area(c):
+            at = (c - HALF + 1) * 4 * CH
+            return late[:, at : at + 4 * CH]
 
-        def high(c, count=1):
-            at = 2 * T + ORDER.index(c) * 2 * CH
-            return mates[:, at : at + count * 2 * CH]
+        def planes_of(c):
+            if c < HALF:
+                return early[:].rearrange("p (j n) -> p j n", j=4)[:, :, c * CH : (c + 1) * CH]
+            return area(c).rearrange("p (j n) -> p j n", j=4)
 
-        def reach(c):
-            return EARLY if c == ORDER[0] else T
-
-        def half(c, t, count=1):
-            return high(c, count).rearrange("p (n t) -> p n t", t=2)[:, :, t]
-
-        held_back = {(ORDER[2], 0): ORDER[4], (ORDER[2], 1): ORDER[5], (ORDER[3], 0): ORDER[6], (ORDER[5], 0): ORDER[7]}
-        for c in held_back.values():
-            nc.vector.memset(high(c)[:, 0:2], 0.0)
-
-        def gather_words(c, count):
+        for j in range(3):
+            cut = HALF * CH - (SHIFT if j == 2 else 0)
+            at = j * HALF * CH
+            nc.scalar.activation(early[:, at : at + cut], raw[j][:].indirect(offsets[:, : cut // 16]), COPY)
+            if cut < HALF * CH:
+                nc.vector.tensor_copy(
+                    out=early[:, at + cut : at + HALF * CH],
+                    in_=raw[j][:].indirect(offsets[:, cut // 16 : HALF * CH // 16]),
+                )
             nc.vector.tensor_copy(
-                out=low(c, count).bitcast(U32), in_=pairs[:, : 2 * reach(c)].bitcast(U32).indirect(slots(c, count))
+                out=late[:, 4 * CH :].rearrange("p (c j n) -> p c j n", j=4, n=CH)[:, :, j, :],
+                in_=raw[j][:].indirect(slots(HALF, HALF)),
             )
 
-        def gather_last(c):
-            nc.scalar.activation(half(c, 1), plane3[:, : reach(c)].indirect(slots(c)), COPY)
-
-        late = {c: held.tile([P, 4 * CH], BF16, name="late" + str(c), align_bytes=64) for c in ORDER[AHEAD:]}
-        both = held.tile([N, 2 * CH], F32, name="both")
-        relu = held.tile([N, CH], F32, name="relu")
-        for c in ORDER[AHEAD:]:
-            nc.vector.memset(late[c][:, 0:2].bitcast(F32), 1.0)
         laced = {}
-        codes = {}
         banks = {}
-        squares = {}
+
+        def gather_last(c):
+            nc.scalar.activation(planes_of(c)[:, 3, :], raw[3][:].indirect(slots(c)), COPY)
 
         def lace(c):
-            on_vector = ORDER.index(c) in V_LACES
-            at = ORDER.index(c) * CH
-            if on_vector:
-                x4 = ring.tile([P, 4 * CH], BF16, name="x4", align_bytes=64, bufs=3)
+            if c < HALF:
+                x4 = ring.tile([P, 4 * CH], BF16, name="x4", align_bytes=64, bufs=HALF)[:]
+                move = nc.vector.tensor_copy
             else:
-                x4 = late[c]
-            engine, word = (nc.vector.tensor_copy, I32) if on_vector else (nc.scalar.copy, U32)
-            engine(
-                out=x4[:].bitcast(word).rearrange("p (n u) -> p n u", u=2),
-                in_=mates[:].bitcast(word).rearrange("p (u n) -> p n u", u=2)[:, at : at + CH, :],
+                x4 = area(c - 1)
+                move = nc.scalar.copy
+            move(
+                out=x4.rearrange("p (c i j) -> p c j i", i=RUN, j=4),
+                in_=planes_of(c).rearrange("p j (c i) -> p c j i", i=RUN),
             )
             laced[c] = x4
 
         def quantise(c):
             cw = ring.tile([P, CH], U32, name="cw", align_bytes=64)
             cs = ring.tile([P, CH], U8, name="cs", align_bytes=64)
-            nc.vector.quantize_mx(out=cw[:].bitcast(FP8X4), scales=cs[:], in_=laced[c][:])
-            codes[c] = (cw, cs)
-
-        def multiply(c):
-            cw, cs = codes[c]
+            nc.vector.quantize_mx(out=cw[:].bitcast(FP8X4), scales=cs[:], in_=laced[c])
             bank = psum.tile([N, CH], F32, name="bank")
             for at, width, e in pieces_of(c):
                 nc.tensor.matmul_mx(
@@ -184,75 +148,66 @@ def tile_moe_rag_lin_relu2_kernel(tc, xT, w_words, w_scales, b, gate, offs, out)
                 )
             banks[c] = bank
 
-        def activate(c):
-            place = ORDER.index(c) + 1
-            if AHEAD <= place < NCH and place not in V_LACES:
-                square = low(ORDER[place]).bitcast(F32)
-            elif place - 1 in (1, 2):
-                square = both[:, (place - 2) * CH : (place - 1) * CH]
-            else:
-                square = ring.tile([N, CH], F32, name="square")[:]
-            for lo, hi, e in spans_of(c):
-                nc.scalar.activation(relu[:, lo:hi], banks[c][:, lo:hi], RELU, bias=b_sb[:, e : e + 1])
-            for n, (lo, hi) in enumerate(((0, CH // 2), (CH // 2, CH))):
-                zero = half(held_back[c, n], 1)[:, 0:1] if (c, n) in held_back else 0.0
-                one = late[ORDER[place + 1]][:, 0:2].bitcast(F32) if n == 0 and AHEAD <= place + 1 < NCH else 1.0
-                nc.scalar.activation(square[:, lo:hi], relu[:, lo:hi], SQUARE, bias=zero, scale=one)
-            squares[c] = square
+        def relu_room(c, h):
+            if c == 0:
+                return spare[:, h * CH // 2 : (h + 1) * CH // 2]
+            if c == 1 and h == 0:
+                return planes_of(5)[:, 3, :].bitcast(F32)
+            if c == 3:
+                return planes_of(6 + h)[:, 3, :].bitcast(F32)
+            room = area({1: 3, 2: 4, 7: 7}.get(c, c + 1))
+            return room[:, h * CH : (h + 1) * CH].bitcast(F32)
 
-        def scatter(c):
-            nc.vector.tensor_tensor(
-                result[:].indirect(slots(c)), squares[c], gate_sb[:, c * CH : (c + 1) * CH], MULT
-            )
+        def rectify(c):
+            for h in range(2):
+                base = c * CH + h * CH // 2
+                for lo, hi, e in expert_spans(base, base + CH // 2):
+                    nc.scalar.activation(
+                        relu_room(c, h)[:, lo - base : hi - base],
+                        banks[c][:, lo - c * CH : hi - c * CH],
+                        RELU,
+                        bias=b_sb[:, e : e + 1],
+                    )
 
-        for lo, hi in zip(CUTS2[:-1], CUTS2[1:]):
-            nc.vector.tensor_copy(out=plane2[:, lo:hi], in_=raw2[:, lo:hi])
-        for c, count in RUNS[:-1]:
-            nc.scalar.activation(half(c, 0, count), plane2[:].indirect(slots(c, count)), COPY)
-        c, count = RUNS[-1]
-        nc.vector.tensor_copy(out=half(c, 0, count), in_=raw2[:].indirect(slots(c, count)))
-        for lo, hi, piece in zip(CUTS01[:-1], CUTS01[1:], raw01):
-            laid = pairs[:, 2 * lo : 2 * hi].rearrange("p (n j) -> p n j", j=2)
-            if 0 < lo < EARLY:
-                nc.vector.tensor_copy(out=laid, in_=piece[:].rearrange("p j n -> p n j"))
-            else:
-                nc.gpsimd.tensor_scalar(laid, piece[:].rearrange("p j n -> p n j"), 1.0, 0.0, MULT, ADD)
-        for c, count in RUNS:
-            gather_words(c, count)
-        for lo, hi, share in zip(CUTS3[:-1], CUTS3[1:], POOL3):
-            if lo == EARLY:
-                gather_last(ORDER[0])
-            cut = lo + share
-            if lo < cut:
-                nc.gpsimd.tensor_scalar(plane3[:, lo:cut], raw3[:, lo:cut], 1.0, 0.0, MULT, ADD)
-            if cut < hi:
-                nc.scalar.copy(out=plane3[:, cut:hi], in_=raw3[:, cut:hi])
+        def square(c):
+            for h in range(2):
+                base = c * CH + h * CH // 2
+                nc.scalar.activation(squares[:, base : base + CH // 2], relu_room(c, h), SQUARE)
 
-        def front(i):
-            lace(ORDER[i])
-            quantise(ORDER[i])
-            multiply(ORDER[i])
+        def scatter(c, count=1):
+            cols = slice(c * CH, (c + count) * CH)
+            nc.vector.tensor_tensor(result[:].indirect(slots(c, count)), squares[:, cols], gate_sb[:, cols], MULT)
 
-        def back(i):
-            activate(ORDER[i])
-            scatter(ORDER[i])
-
-        for i in range(AHEAD):
-            if i > 0:
-                gather_last(ORDER[i])
-            front(i)
-        back(0)
-        activate(ORDER[1])
-        activate(ORDER[2])
-        c = ORDER[1]
-        nc.vector.tensor_tensor(result[:].indirect(slots(c, 2)), both[:], gate_sb[:, c * CH : (c + 2) * CH], MULT)
-        gather_last(ORDER[AHEAD])
-        for i in range(2, NCH):
-            if i > 2:
-                back(i)
-            if i != 4 and i + 2 < NCH:
-                gather_last(ORDER[min(i + LAG, NCH - 1)])
-            if i + 2 < NCH:
-                front(i + 2)
-        for queue, lo in ((nc.sync, 0), (nc.scalar, 2048)):
-            queue.dma_start(out=out[:, lo : lo + 2048], in_=result[:, lo : lo + 2048])
+        for c in range(HALF + 1):
+            gather_last(c)
+        lace(0)
+        for c in range(HALF):
+            if c + 1 < HALF:
+                lace(c + 1)
+            quantise(c)
+        for c in range(2):
+            rectify(c)
+            square(c)
+        gather_last(5)
+        lace(4)
+        scatter(0, 2)
+        quantise(4)
+        rectify(2)
+        rectify(3)
+        square(2)
+        square(3)
+        gather_last(6)
+        gather_last(7)
+        lace(5)
+        scatter(2, 2)
+        quantise(5)
+        for c in range(HALF, NCH):
+            rectify(c)
+            square(c)
+            if c + 2 < NCH:
+                lace(c + 2)
+            scatter(c)
+            if c + 2 < NCH:
+                quantise(c + 2)
+        for queue, lo in ((nc.sync, 0), (nc.scalar, T // 2)):
+            queue.dma_start(out=out[:, lo : lo + T // 2], in_=result[:, lo : lo + T // 2])

@@ -20,6 +20,7 @@ CH = 512
 NCH = T // CH
 HALF = NCH // 2
 RUN = 4
+ORDER = (0, 1, 2, 3, 6, 7, 4, 5)
 SHIFT = 256
 
 
@@ -34,7 +35,8 @@ def expert_spans(lo, hi):
     return found
 
 
-def pieces_of(c):
+def pieces_of(i):
+    c = ORDER[i]
     found = []
     for lo, hi, e in expert_spans(c * CH, (c + 1) * CH):
         while lo < hi:
@@ -77,20 +79,22 @@ def tile_moe_rag_lin_relu2_kernel(tc, xT, w_words, w_scales, b, gate, offs, out)
                 in_=w_scales[:, 0, 4 * q : 4 * q + 4, :].rearrange("e q n -> q e n").bitcast(I32),
             )
         nc.sync.dma_start(out=b_sb[:], in_=b)
-        for lo in range(0, T, 2 * CH):
+        for lo in [ORDER[i] * CH for i in range(0, NCH, 2)]:
             nc.sync.dma_start(out=gate_sb[:, lo : lo + 2 * CH], in_=gate[:, lo : lo + 2 * CH])
 
         early = held.tile([P, 4 * HALF * CH], BF16, name="early", align_bytes=64)
-        late = held.tile([P, (HALF + 1) * 4 * CH], BF16, name="late", align_bytes=64)
+        late = held.tile([P, HALF * 4 * CH], BF16, name="late", align_bytes=64)
+        woven = held.tile([P, HALF * 4 * CH + 3 * CH // 2], BF16, name="woven", align_bytes=64)
+        woven_at = {4: 0, 5: 4 * CH, 6: 9 * CH, 7: 13 * CH + CH // 2}
         spare = held.tile([P, CH], F32, name="spare")
         squares = held.tile([N, T], F32, name="squares")
         result = held.tile([P, T], F32, name="result")
 
-        def slots(c, count=1):
-            return offsets[:, c * CH // 16 : (c + count) * CH // 16]
+        def slots(i, count=1):
+            return offsets[:, ORDER[i] * CH // 16 : (ORDER[i] + count) * CH // 16]
 
         def area(c):
-            at = (c - HALF + 1) * 4 * CH
+            at = (ORDER[c] - HALF) * 4 * CH
             return late[:, at : at + 4 * CH]
 
         def planes_of(c):
@@ -108,8 +112,8 @@ def tile_moe_rag_lin_relu2_kernel(tc, xT, w_words, w_scales, b, gate, offs, out)
                     in_=raw[j][:].indirect(offsets[:, cut // 16 : HALF * CH // 16]),
                 )
             nc.vector.tensor_copy(
-                out=late[:, 4 * CH :].rearrange("p (c j n) -> p c j n", j=4, n=CH)[:, :, j, :],
-                in_=raw[j][:].indirect(slots(HALF, HALF)),
+                out=late[:].rearrange("p (c j n) -> p c j n", j=4, n=CH)[:, :, j, :],
+                in_=raw[j][:].indirect(offsets[:, HALF * CH // 16 :]),
             )
 
         laced = {}
@@ -118,23 +122,25 @@ def tile_moe_rag_lin_relu2_kernel(tc, xT, w_words, w_scales, b, gate, offs, out)
         def gather_last(c):
             nc.scalar.activation(planes_of(c)[:, 3, :], raw[3][:].indirect(slots(c)), COPY)
 
-        def lace(c):
-            if c < HALF:
-                x4 = ring.tile([P, 4 * CH], BF16, name="x4", align_bytes=64, bufs=HALF)[:]
-                move = nc.vector.tensor_copy
-            else:
-                x4 = area(c - 1)
-                move = nc.scalar.copy
+        def lace(c, move, lo=0, hi=CH):
+            if c not in laced:
+                if c < HALF:
+                    laced[c] = ring.tile([P, 4 * CH], BF16, name="x4", align_bytes=64, bufs=HALF)[:]
+                else:
+                    laced[c] = woven[:, woven_at[c] : woven_at[c] + 4 * CH]
             move(
-                out=x4.rearrange("p (c i j) -> p c j i", i=RUN, j=4),
-                in_=planes_of(c).rearrange("p j (c i) -> p c j i", i=RUN),
+                out=laced[c][:, 4 * lo : 4 * hi].rearrange("p (c i j) -> p c j i", i=RUN, j=4),
+                in_=planes_of(c)[:, :, lo:hi].rearrange("p j (c i) -> p c j i", i=RUN),
             )
-            laced[c] = x4
 
-        def quantise(c):
+        def quantise(c, parts=1):
             cw = ring.tile([P, CH], U32, name="cw", align_bytes=64)
             cs = ring.tile([P, CH], U8, name="cs", align_bytes=64)
-            nc.vector.quantize_mx(out=cw[:].bitcast(FP8X4), scales=cs[:], in_=laced[c])
+            for lo in range(0, CH, CH // parts):
+                hi = lo + CH // parts
+                nc.vector.quantize_mx(
+                    out=cw[:, lo:hi].bitcast(FP8X4), scales=cs[:, lo:hi], in_=laced[c][:, 4 * lo : 4 * hi]
+                )
             bank = psum.tile([N, CH], F32, name="bank")
             for at, width, e in pieces_of(c):
                 nc.tensor.matmul_mx(
@@ -148,64 +154,88 @@ def tile_moe_rag_lin_relu2_kernel(tc, xT, w_words, w_scales, b, gate, offs, out)
                 )
             banks[c] = bank
 
-        def relu_room(c, h):
+        def rooms(c):
+            half, quarter = CH // 2, CH // 4
+            words = woven[:].bitcast(F32)
+            wide, narrow = woven_at[5] // 2 + 2 * CH, woven_at[6] // 2 + 2 * CH
             if c == 0:
-                return spare[:, h * CH // 2 : (h + 1) * CH // 2]
-            if c == 1 and h == 0:
-                return planes_of(5)[:, 3, :].bitcast(F32)
+                return [(0, half, spare[:, :half]), (half, CH, spare[:, half:])]
+            if c == 1:
+                return [(0, half, words[:, 2 * CH - half : 2 * CH]), (half, CH, planes_of(5)[:, 3, :].bitcast(F32))]
+            if c == 2:
+                return [
+                    (0, 3 * quarter, words[:, wide - quarter : wide + half]),
+                    (3 * quarter, CH, words[:, narrow : narrow + quarter]),
+                ]
             if c == 3:
-                return planes_of(6 + h)[:, 3, :].bitcast(F32)
-            room = area({1: 3, 2: 4, 7: 7}.get(c, c + 1))
-            return room[:, h * CH : (h + 1) * CH].bitcast(F32)
+                rows_f32 = late[:].bitcast(F32).rearrange("p (c n) -> p c n", c=HALF)
+                return [(0, CH, rows_f32[:, 0:2, 3 * half :])]
+            at = narrow if c == 5 else narrow - quarter
+            front = words[:, at : at + half].rearrange("p (r n) -> p r n", r=2)
+            return [(0, half, front), (half, CH, words[:, wide : wide + half])]
+
+        def parts(c):
+            first = ORDER[c] * CH
+            found = []
+            for lo, hi, room in rooms(c):
+                rows_n = room.shape[1] if len(room.shape) == 3 else 1
+                for a, z, e in expert_spans(first + lo, first + hi):
+                    cols = slice((a - first - lo) // rows_n, (z - first - lo) // rows_n)
+                    found.append((a, z, e, room[:, :, cols] if rows_n > 1 else room[:, cols]))
+            return found
+
+        def like(room, ap):
+            return ap.rearrange("p (r n) -> p r n", r=room.shape[1]) if len(room.shape) == 3 else ap
 
         def rectify(c):
-            for h in range(2):
-                base = c * CH + h * CH // 2
-                for lo, hi, e in expert_spans(base, base + CH // 2):
-                    nc.scalar.activation(
-                        relu_room(c, h)[:, lo - base : hi - base],
-                        banks[c][:, lo - c * CH : hi - c * CH],
-                        RELU,
-                        bias=b_sb[:, e : e + 1],
-                    )
+            first = ORDER[c] * CH
+            for a, z, e, room in parts(c):
+                nc.scalar.activation(room, like(room, banks[c][:, a - first : z - first]), RELU, bias=b_sb[:, e : e + 1])
 
         def square(c):
-            for h in range(2):
-                base = c * CH + h * CH // 2
-                nc.scalar.activation(squares[:, base : base + CH // 2], relu_room(c, h), SQUARE)
+            first = ORDER[c] * CH
+            for lo, hi, room in rooms(c):
+                to = squares[:, first + lo : first + hi]
+                count = len(expert_spans(first + lo, first + hi))
+                if len(room.shape) == 3:
+                    to = to.rearrange("p (s r n) -> p s r n", s=count, r=room.shape[1])
+                    room = room.rearrange("p r (s n) -> p s r n", s=count)
+                nc.scalar.activation(to, room, SQUARE)
 
         def scatter(c, count=1):
-            cols = slice(c * CH, (c + count) * CH)
+            cols = slice(ORDER[c] * CH, (ORDER[c] + count) * CH)
             nc.vector.tensor_tensor(result[:].indirect(slots(c, count)), squares[:, cols], gate_sb[:, cols], MULT)
 
         for c in range(HALF + 1):
             gather_last(c)
-        lace(0)
+        on_vector, on_scalar = nc.vector.tensor_copy, nc.scalar.copy
+        lace(0, on_vector)
         for c in range(HALF):
             if c + 1 < HALF:
-                lace(c + 1)
+                lace(c + 1, on_vector)
             quantise(c)
         for c in range(2):
             rectify(c)
             square(c)
+        lace(4, on_scalar)
         gather_last(5)
-        lace(4)
         scatter(0, 2)
         quantise(4)
         rectify(2)
         rectify(3)
         square(2)
         square(3)
+        lace(5, on_scalar)
         gather_last(6)
-        gather_last(7)
-        lace(5)
         scatter(2, 2)
         quantise(5)
         for c in range(HALF, NCH):
             rectify(c)
             square(c)
             if c + 2 < NCH:
-                lace(c + 2)
+                lace(c + 2, on_scalar)
+            if c == HALF:
+                gather_last(7)
             scatter(c)
             if c + 2 < NCH:
                 quantise(c + 2)

@@ -103,14 +103,9 @@ def tile_moe_rag_lin_relu2_kernel(tc, xT, w_words, w_scales, b, gate, offs, out)
             return area(c).rearrange("p (j n) -> p j n", j=4)
 
         for j in range(3):
-            cut = HALF * CH - (SHIFT if j == 2 else 0)
-            at = j * HALF * CH
-            nc.scalar.activation(early[:, at : at + cut], raw[j][:].indirect(offsets[:, : cut // 16]), COPY)
-            if cut < HALF * CH:
-                nc.vector.tensor_copy(
-                    out=early[:, at + cut : at + HALF * CH],
-                    in_=raw[j][:].indirect(offsets[:, cut // 16 : HALF * CH // 16]),
-                )
+            nc.scalar.activation(
+                early[:, j * HALF * CH : (j + 1) * HALF * CH], raw[j][:].indirect(slots(0, HALF)), COPY
+            )
             nc.vector.tensor_copy(
                 out=late[:].rearrange("p (c j n) -> p c j n", j=4, n=CH)[:, :, j, :],
                 in_=raw[j][:].indirect(offsets[:, HALF * CH // 16 :]),
@@ -206,7 +201,10 @@ def tile_moe_rag_lin_relu2_kernel(tc, xT, w_words, w_scales, b, gate, offs, out)
             cols = slice(ORDER[c] * CH, (ORDER[c] + count) * CH)
             nc.vector.tensor_tensor(result[:].indirect(slots(c, count)), squares[:, cols], gate_sb[:, cols], MULT)
 
-        for c in range(HALF + 1):
+        first = planes_of(0)[:, 3, :]
+        nc.vector.tensor_copy(out=first[:, :SHIFT], in_=raw[3][:].indirect(slots(0)[:, : SHIFT // 16]))
+        nc.scalar.activation(first[:, SHIFT:], raw[3][:].indirect(slots(0)[:, SHIFT // 16 :]), COPY)
+        for c in range(1, HALF + 1):
             gather_last(c)
         on_vector, on_scalar = nc.vector.tensor_copy, nc.scalar.copy
         lace(0, on_vector)

import concourse.mybir as mybir

F32 = mybir.dt.float32
BF16 = mybir.dt.bfloat16
U32 = mybir.dt.uint32
I32 = mybir.dt.int32
U16 = mybir.dt.uint16
U8 = mybir.dt.uint8
FP8X4 = mybir.dt.float8_e4m3fn_x4
FP4X4 = mybir.dt.float4_e2m1fn_x4
RELU = mybir.ActivationFunctionType.Relu
COPY = mybir.ActivationFunctionType.Copy
SQUARE = mybir.ActivationFunctionType.Square
MULT = mybir.AluOpType.mult

P, T, E, N, K = 128, 4096, 8, 128, 512
COUNTS = (128, 128, 512, 640, 896, 896, 384, 512)
FLOPS = 2 * K * N * T
CH = 512
NCH = T // CH
HALF = NCH // 2
RUN = 4
ORDER = (0, 1, 2, 3, 6, 7, 4, 5)
SHIFT = 256


def expert_spans(lo, hi):
    found = []
    start = 0
    for e in range(E):
        a, z = max(start, lo), min(start + COUNTS[e], hi)
        start += COUNTS[e]
        if a < z:
            found.append((a, z, e))
    return found


def pieces_of(i):
    c = ORDER[i]
    found = []
    for lo, hi, e in expert_spans(c * CH, (c + 1) * CH):
        while lo < hi:
            width = max(n for n in (128, 256, 512) if n <= hi - lo)
            found.append((lo - c * CH, width, e))
            lo += width
    return found


def tile_moe_rag_lin_relu2_kernel(tc, xT, w_words, w_scales, b, gate, offs, out):
    nc = tc.nc
    with (
        tc.tile_pool(name="held", bufs=1) as held,
        tc.tile_pool(name="ring", bufs=NCH) as ring,
        tc.psum_pool(name="psum", bufs=NCH) as psum,
    ):
        offsets = held.tile([P, T // 16], U16, name="offsets")
        w_sb = held.tile([P, E, 2 * N], U8, name="w_sb", align_bytes=64)
        ws_sb = held.tile([P, E, N], U8, name="ws_sb", align_bytes=64)
        b_sb = held.tile([P, E], F32, name="b_sb")
        gate_sb = held.tile([P, T], F32, name="gate_sb")
        nc.vector.memset(ws_sb[:].rearrange("p e n -> p (e n)").bitcast(I32), 0)

        warm = held.tile([P, 2], F32, name="warm")
        nc.vector.memset(warm[:, 0:1], 0.0)
        nc.scalar.activation(warm[:, 1:2], warm[:, 0:1], SQUARE)

        rows = xT.rearrange("(p j) n -> p j n", j=4)
        raw = []
        for j in range(4):
            plane = held.tile([P, T], F32, name="raw" + str(j))
            nc.sync.dma_start(out=plane[:], in_=rows[:, j, :])
            if j == 0:
                nc.sync.dma_start(offsets[:], offs)
            raw.append(plane)
        nc.sync.dma_start(out=w_sb[:].bitcast(I32), in_=w_words[:, 0].rearrange("e p n -> p e n").bitcast(I32))
        for q in range(4):
            nc.sync.dma_start(
                out=ws_sb[32 * q : 32 * q + 4].bitcast(I32),
                in_=w_scales[:, 0, 4 * q : 4 * q + 4, :].rearrange("e q n -> q e n").bitcast(I32),
            )
        nc.sync.dma_start(out=b_sb[:], in_=b)
        for lo in [ORDER[i] * CH for i in range(0, NCH, 2)]:
            nc.sync.dma_start(out=gate_sb[:, lo : lo + 2 * CH], in_=gate[:, lo : lo + 2 * CH])

        early = held.tile([P, 4 * HALF * CH], BF16, name="early", align_bytes=64)
        late = held.tile([P, HALF * 4 * CH], BF16, name="late", align_bytes=64)
        woven = held.tile([P, HALF * 4 * CH + 3 * CH // 2], BF16, name="woven", align_bytes=64)
        woven_at = {4: 0, 5: 4 * CH, 6: 9 * CH, 7: 13 * CH + CH // 2}
        spare = held.tile([P, CH], F32, name="spare")
        squares = held.tile([N, T], F32, name="squares")
        result = held.tile([P, T], F32, name="result")

        def slots(i, count=1):
            return offsets[:, ORDER[i] * CH // 16 : (ORDER[i] + count) * CH // 16]

        def area(c):
            at = (ORDER[c] - HALF) * 4 * CH
            return late[:, at : at + 4 * CH]

        def planes_of(c):
            if c < HALF:
                return early[:].rearrange("p (j n) -> p j n", j=4)[:, :, c * CH : (c + 1) * CH]
            return area(c).rearrange("p (j n) -> p j n", j=4)

        for j in range(3):
            nc.scalar.activation(
                early[:, j * HALF * CH : (j + 1) * HALF * CH], raw[j][:].indirect(slots(0, HALF)), COPY
            )
            nc.vector.tensor_copy(
                out=late[:].rearrange("p (c j n) -> p c j n", j=4, n=CH)[:, :, j, :],
                in_=raw[j][:].indirect(offsets[:, HALF * CH // 16 :]),
            )

        laced = {}
        banks = {}

        def gather_last(c):
            nc.scalar.activation(planes_of(c)[:, 3, :], raw[3][:].indirect(slots(c)), COPY)

        def lace(c, move, lo=0, hi=CH):
            if c not in laced:
                if c < HALF:
                    laced[c] = ring.tile([P, 4 * CH], BF16, name="x4", align_bytes=64, bufs=HALF)[:]
                else:
                    laced[c] = woven[:, woven_at[c] : woven_at[c] + 4 * CH]
            move(
                out=laced[c][:, 4 * lo : 4 * hi].rearrange("p (c i j) -> p c j i", i=RUN, j=4),
                in_=planes_of(c)[:, :, lo:hi].rearrange("p j (c i) -> p c j i", i=RUN),
            )

        def quantise(c, parts=1):
            cw = ring.tile([P, CH], U32, name="cw", align_bytes=64)
            cs = ring.tile([P, CH], U8, name="cs", align_bytes=64)
            for lo in range(0, CH, CH // parts):
                hi = lo + CH // parts
                nc.vector.quantize_mx(
                    out=cw[:, lo:hi].bitcast(FP8X4), scales=cs[:, lo:hi], in_=laced[c][:, 4 * lo : 4 * hi]
                )
            bank = psum.tile([N, CH], F32, name="bank")
            for at, width, e in pieces_of(c):
                nc.tensor.matmul_mx(
                    out=bank[:, at : at + width],
                    lhsT=w_sb[:, e, :].bitcast(FP4X4),
                    lhsT_scale=ws_sb[:, e, :],
                    rhs=cw[:, at : at + width].bitcast(FP8X4),
                    rhs_scale=cs[:, at : at + width],
                    start=True,
                    stop=True,
                )
            banks[c] = bank

        def rooms(c):
            half, quarter = CH // 2, CH // 4
            words = woven[:].bitcast(F32)
            wide, narrow = woven_at[5] // 2 + 2 * CH, woven_at[6] // 2 + 2 * CH
            if c == 0:
                return [(0, half, spare[:, :half]), (half, CH, spare[:, half:])]
            if c == 1:
                return [(0, half, words[:, 2 * CH - half : 2 * CH]), (half, CH, planes_of(5)[:, 3, :].bitcast(F32))]
            if c == 2:
                return [
                    (0, 3 * quarter, words[:, wide - quarter : wide + half]),
                    (3 * quarter, CH, words[:, narrow : narrow + quarter]),
                ]
            if c == 3:
                rows_f32 = late[:].bitcast(F32).rearrange("p (c n) -> p c n", c=HALF)
                return [(0, CH, rows_f32[:, 0:2, 3 * half :])]
            at = narrow if c == 5 else narrow - quarter
            front = words[:, at : at + half].rearrange("p (r n) -> p r n", r=2)
            return [(0, half, front), (half, CH, words[:, wide : wide + half])]

        def parts(c):
            first = ORDER[c] * CH
            found = []
            for lo, hi, room in rooms(c):
                rows_n = room.shape[1] if len(room.shape) == 3 else 1
                for a, z, e in expert_spans(first + lo, first + hi):
                    cols = slice((a - first - lo) // rows_n, (z - first - lo) // rows_n)
                    found.append((a, z, e, room[:, :, cols] if rows_n > 1 else room[:, cols]))
            return found

        def like(room, ap):
            return ap.rearrange("p (r n) -> p r n", r=room.shape[1]) if len(room.shape) == 3 else ap

        def rectify(c):
            first = ORDER[c] * CH
            for a, z, e, room in parts(c):
                nc.scalar.activation(room, like(room, banks[c][:, a - first : z - first]), RELU, bias=b_sb[:, e : e + 1])

        def square(c):
            first = ORDER[c] * CH
            for lo, hi, room in rooms(c):
                to = squares[:, first + lo : first + hi]
                count = len(expert_spans(first + lo, first + hi))
                if len(room.shape) == 3:
                    to = to.rearrange("p (s r n) -> p s r n", s=count, r=room.shape[1])
                    room = room.rearrange("p r (s n) -> p s r n", s=count)
                nc.scalar.activation(to, room, SQUARE)

        def scatter(c, count=1):
            cols = slice(ORDER[c] * CH, (ORDER[c] + count) * CH)
            nc.vector.tensor_tensor(result[:].indirect(slots(c, count)), squares[:, cols], gate_sb[:, cols], MULT)

        first = planes_of(0)[:, 3, :]
        nc.vector.tensor_copy(out=first[:, :SHIFT], in_=raw[3][:].indirect(slots(0)[:, : SHIFT // 16]))
        nc.scalar.activation(first[:, SHIFT:], raw[3][:].indirect(slots(0)[:, SHIFT // 16 :]), COPY)
        for c in range(1, HALF + 1):
            gather_last(c)
        on_vector, on_scalar = nc.vector.tensor_copy, nc.scalar.copy
        lace(0, on_vector)
        for c in range(HALF):
            if c + 1 < HALF:
                lace(c + 1, on_vector)
            quantise(c)
        for c in range(2):
            rectify(c)
            square(c)
        lace(4, on_scalar)
        gather_last(5)
        scatter(0, 2)
        quantise(4)
        rectify(2)
        rectify(3)
        square(2)
        square(3)
        lace(5, on_scalar)
        gather_last(6)
        scatter(2, 2)
        quantise(5)
        for c in range(HALF, NCH):
            rectify(c)
            square(c)
            if c + 2 < NCH:
                lace(c + 2, on_scalar)
            if c == HALF:
                gather_last(7)
            scatter(c)
            if c + 2 < NCH:
                quantise(c + 2)
        for queue, lo in ((nc.sync, 0), (nc.scalar, T // 2)):
            queue.dma_start(out=out[:, lo : lo + T // 2], in_=result[:, lo : lo + T // 2])
